import numpy as np
import ml_dtypes


def mxq(x, axis, fmt="e4m3"):
    dtype, down = {"e4m3": (ml_dtypes.float8_e4m3fn, 7), "e5m2": (ml_dtypes.float8_e5m2, 14)}[fmt]
    v = np.moveaxis(np.asarray(x, np.float32).astype(ml_dtypes.bfloat16).astype(np.float64), axis, -1)
    blocks = v.reshape(v.shape[:-1] + (-1, 32))
    amax = np.abs(blocks).max(-1, keepdims=True)
    byte = np.maximum(np.where(amax > 0, np.frexp(amax)[1] - 1 + 127, 0) - down, 1)
    scale = np.exp2(byte - 127.0)
    codes = (blocks / scale).astype(np.float32).astype(dtype).astype(np.float64)
    return np.moveaxis((codes * scale).reshape(v.shape), -1, axis)


WIDE = False


def mx_kscale(k):
    if not WIDE:
        return np.ones(k)
    levels = np.array([10, -10, 5, -5, 0])
    if k % 512:
        return np.exp2(np.random.permutation(np.resize(levels, k // 32))).repeat(32)
    a = np.empty((k // 512, 16))
    for p in range(k // 512):
        a[p, :8] = np.random.permutation(np.resize(levels, 8))
        for g in range(8):
            far = levels[np.abs(levels - a[p, g]) >= 10]
            a[p, g + 8] = far[np.random.randint(len(far))]
    return np.exp2(a.ravel()).repeat(32)


def f64(x):
    return np.asarray(x).astype(np.float64)


def striped(idx):
    return np.tile(idx.reshape(-1, 16).T, (8, 1)).astype(np.uint16)


def unstriped(offs):
    return offs[:16].T.reshape(-1).astype(np.int64)


def pack_weight(w):
    k, n = w.shape
    w = f64(np.asarray(w, np.float32).astype(ml_dtypes.bfloat16)).reshape(k // 32, 32, n)
    amax = np.abs(w).max(1)
    byte = np.clip(np.where(amax > 0, np.frexp(amax)[1] - 1 + 127 - 7, 1), 1, 254)
    scaled = (w * np.exp2(127.0 - byte)[:, None, :]).reshape(k, n).astype(np.float32)
    words = np.ascontiguousarray(scaled.reshape(k // 512, 128, 4, n).transpose(0, 1, 3, 2)).astype(ml_dtypes.float8_e4m3fn).view(np.uint8)
    return words, np.ascontiguousarray(byte.astype(np.uint8).reshape(k // 512, 16, n))


def unpack_weight(words, scales):
    g, p, n, _ = words.shape
    vals = np.ascontiguousarray(words).view(ml_dtypes.float8_e4m3fn).astype(np.float64) * np.repeat(np.exp2(scales.astype(np.float64) - 127.0), 8, axis=1)[..., None]
    return vals.transpose(0, 1, 3, 2).reshape(g * 512, n)


def relu(v):
    return np.maximum(v, 0.0)


def sigmoid(v):
    return 1.0 / (1.0 + np.exp(-np.maximum(v, -700.0)))


K, T, S, N = 1024, 1024, 512, 128


def setup_inputs():
    n = np.random.standard_normal
    s = mx_kscale(K)[:, None]
    packed_xT = pack_weight(n((K, T)) * s)
    return {
        "x_words": packed_xT[0],
        "x_scales": packed_xT[1],
        "res": n((N, T)).astype(np.float32),
        "w1": (n((K, N)) / np.sqrt(K) / s).astype(np.float32),
        "w2": (n((K, N)) / np.sqrt(K) / s).astype(np.float32),
        "offs": striped(np.random.permutation(T)[:S]),
    }


def reference(x_words, x_scales, res, w1, w2, offs):
    r = f64(res)[:, unstriped(offs)]
    xq = unpack_weight(x_words, x_scales)[:, unstriped(offs)]
    g = sigmoid(mxq(f64(w2), 0, "e4m3").T @ xq)
    y = relu(mxq(f64(w1), 0, "e4m3").T @ xq)
    return r + g * (y - r)

@@ -1,0 +1,130 @@
+from contextlib import ExitStack
+
+import concourse.mybir as mybir
+
+K, T, S, N = 1024, 1024, 512, 128
+FLOPS = 2 * 2 * K * N * S
+
+F32 = mybir.dt.float32
+BF16 = mybir.dt.bfloat16
+I32 = mybir.dt.int32
+U32 = mybir.dt.uint32
+U16 = mybir.dt.uint16
+U8 = mybir.dt.uint8
+FP8X4 = mybir.dt.float8_e4m3fn_x4
+ACT = mybir.ActivationFunctionType
+ALU = mybir.AluOpType
+
+P = 128
+PACK = 4
+K_PASS = P * PACK
+PASSES = K // K_PASS
+HALVES = 2
+H = S // HALVES
+LIST_COLS = 16
+
+
+def tile_picked_highway_relu_p_kernel(tc, x_words, x_scales, res, w1, w2, offs, out):
+    nc = tc.nc
+    with ExitStack() as ctx:
+        sb = ctx.enter_context(tc.tile_pool(name="sb", bufs=1))
+        ps = ctx.enter_context(tc.psum_pool(name="ps", bufs=1))
+
+        offsets = sb.tile([P, S // LIST_COLS], U16, name="offsets")
+        nc.sync.dma_start(offsets[:], offs)
+
+        scale_tab = sb.tile([P, T], U8, name="scale_tab", align_bytes=64)
+        nc.vector.memset(scale_tab[:].bitcast(I32), 0)
+
+        warm_in = sb.tile([P, 8], F32, name="warm_in")
+        warm_out = sb.tile([P, 8], F32, name="warm_out")
+        nc.vector.memset(warm_in[:], 0.0)
+        nc.scalar.activation(warm_out[:], warm_in[:], ACT.Sigmoid)
+
+        word_tab, raw = {}, {}
+
+        def load_words(z):
+            tab = sb.tile([P, T], I32, name=f"word_tab{z}", align_bytes=64)
+            nc.sync.dma_start(tab[:], x_words[z].rearrange("p c r -> p (c r)").bitcast(I32))
+            word_tab[z] = tab
+
+        def load_weights(name, w, z):
+            t = sb.tile([P, PACK, N], F32, name=f"raw_{name}{z}", align_bytes=64)
+            nc.sync.dma_start(t[:], w[z * K_PASS : (z + 1) * K_PASS, :].rearrange("(p j) m -> p j m", j=PACK))
+            raw[name, z] = t
+
+        load_words(0)
+        scales_i32 = x_scales.bitcast(I32)
+        for q in range(4):
+            nc.sync.dma_start(
+                scale_tab[32 * q : 32 * q + 4 * PASSES, :].bitcast(I32),
+                scales_i32[:, 4 * q : 4 * q + 4, :],
+            )
+        load_weights("g", w2, 0)
+        load_words(1)
+        load_weights("g", w2, 1)
+        for z in range(PASSES):
+            load_weights("y", w1, z)
+
+        res_tab = sb.tile([P, T], F32, name="res_tab", align_bytes=64)
+        nc.sync.dma_start(res_tab[:], res)
+
+        x_sc = sb.tile([P, S], U8, name="x_sc", align_bytes=64)
+        nc.vector.tensor_copy(x_sc[:], scale_tab[:].indirect(offsets[:]))
+        x_codes = []
+        for z in range(PASSES):
+            c = sb.tile([P, S], U32, name=f"x_codes{z}", align_bytes=64)
+            nc.vector.tensor_copy(c[:], word_tab[z][:].bitcast(U32).indirect(offsets[:]))
+            x_codes.append(c)
+
+        acc = {}
+        for name in ("g", "y"):
+            for h in range(HALVES):
+                acc[name, h] = ps.tile([P, H], F32, name=f"acc_{name}{h}")
+            for z in range(PASSES):
+                grouped = sb.tile([P, N, PACK], BF16, name=f"grouped_{name}{z}", align_bytes=64)
+                nc.scalar.copy(
+                    grouped[:].rearrange("p (c i) t -> p c t i", i=4),
+                    raw[name, z][:].rearrange("p t (c i) -> p c t i", i=4),
+                )
+                codes = sb.tile([P, N], U32, name=f"w_codes_{name}{z}", align_bytes=64)
+                scales = sb.tile([P, N], U8, name=f"w_scales_{name}{z}", align_bytes=64)
+                nc.vector.quantize_mx(
+                    out=codes[:].bitcast(FP8X4),
+                    scales=scales[:],
+                    in_=grouped[:].rearrange("p m t -> p (m t)"),
+                )
+                for h in range(HALVES):
+                    cols = slice(h * H, (h + 1) * H)
+                    nc.tensor.matmul_mx(
+                        out=acc[name, h][:],
+                        lhsT=codes[:].bitcast(FP8X4),
+                        lhsT_scale=scales[:],
+                        rhs=x_codes[z][:, cols].bitcast(FP8X4),
+                        rhs_scale=x_sc[4 * z : P, cols],
+                        start=(z == 0),
+                        stop=(z == PASSES - 1),
+                    )
+
+        carry, gate, passed, layer = [], [], [], []
+        for h in range(HALVES):
+            c = sb.tile([P, H], F32, name=f"carry{h}")
+            nc.scalar.activation(c[:], acc["g", h][:], ACT.Sigmoid, scale=-1.0)
+            carry.append(c)
+        for h in range(HALVES):
+            g = sb.tile([P, H], F32, name=f"gate{h}")
+            nc.scalar.activation(g[:], acc["g", h][:], ACT.Sigmoid)
+            gate.append(g)
+        for h in range(HALVES):
+            t = sb.tile([P, H], F32, name=f"passed{h}")
+            piece = offsets[:, h * H // LIST_COLS : (h + 1) * H // LIST_COLS]
+            nc.vector.tensor_tensor(t[:], res_tab[:].indirect(piece), carry[h][:], ALU.mult)
+            passed.append(t)
+        for h in range(HALVES):
+            a = sb.tile([P, H], F32, name=f"layer{h}")
+            nc.vector.scalar_tensor_tensor(a[:], acc["y", h][:], 0.0, gate[h][:], ALU.max, ALU.mult)
+            layer.append(a)
+        for h in range(HALVES):
+            o = sb.tile([P, H], F32, name=f"result{h}")
+            nc.vector.tensor_tensor(o[:], layer[h][:], passed[h][:], ALU.add)
+            nc.sync.dma_start(out[:, h * H : (h + 1) * H], o[:])

@@ -61,67 +61,82 @@ def tile_picked_highway_relu_p_kernel(tc, x_words, x_scales, res, w1, w2, offs, 
                 scales_i32[:, 4 * q : 4 * q + 4, :],
             )
         load_weights("g", w2, 0)
-        load_words(1)
         load_weights("g", w2, 1)
+        load_words(1)
         for z in range(PASSES):
             load_weights("y", w1, z)
 
         res_tab = sb.tile([P, T], F32, name="res_tab", align_bytes=64)
         nc.sync.dma_start(res_tab[:], res)
 
+        pieces = [offsets[:, h * H // LIST_COLS : (h + 1) * H // LIST_COLS] for h in range(HALVES)]
+        x_codes = {}
+        c = sb.tile([P, S], U32, name="x_codes0", align_bytes=64)
+        nc.vector.tensor_copy(c[:], word_tab[0][:].bitcast(U32).indirect(offsets[:]))
+        for h in range(HALVES):
+            x_codes[0, h] = c[:, h * H : (h + 1) * H]
         x_sc = sb.tile([P, S], U8, name="x_sc", align_bytes=64)
         nc.vector.tensor_copy(x_sc[:], scale_tab[:].indirect(offsets[:]))
-        x_codes = []
-        for z in range(PASSES):
-            c = sb.tile([P, S], U32, name=f"x_codes{z}", align_bytes=64)
-            nc.vector.tensor_copy(c[:], word_tab[z][:].bitcast(U32).indirect(offsets[:]))
-            x_codes.append(c)
 
-        acc = {}
-        for name in ("g", "y"):
+        w_codes, w_scales = {}, {}
+
+        def quantise(name, z):
+            grouped = sb.tile([P, N, PACK], BF16, name=f"grouped_{name}{z}", align_bytes=64)
+            cast = nc.vector.tensor_copy if (name, z) == ("y", PASSES - 1) else nc.scalar.copy
+            cast(
+                grouped[:].rearrange("p (c i) t -> p c t i", i=4),
+                raw[name, z][:].rearrange("p t (c i) -> p c t i", i=4),
+            )
+            codes = sb.tile([P, N], U32, name=f"w_codes_{name}{z}", align_bytes=64)
+            scales = sb.tile([P, N], U8, name=f"w_scales_{name}{z}", align_bytes=64)
+            nc.vector.quantize_mx(
+                out=codes[:].bitcast(FP8X4),
+                scales=scales[:],
+                in_=grouped[:].rearrange("p m t -> p (m t)"),
+            )
+            w_codes[name, z], w_scales[name, z] = codes, scales
+
+        acc = {(name, h): ps.tile([P, H], F32, name=f"acc_{name}{h}") for name in ("g", "y") for h in range(HALVES)}
+
+        def multiply(name, z, h):
+            nc.tensor.matmul_mx(
+                out=acc[name, h][:],
+                lhsT=w_codes[name, z][:].bitcast(FP8X4),
+                lhsT_scale=w_scales[name, z][:],
+                rhs=x_codes[z, h].bitcast(FP8X4),
+                rhs_scale=x_sc[4 * z : P, h * H : (h + 1) * H],
+                start=(z == 0),
+                stop=(z == PASSES - 1),
+            )
+
+        quantise("g", 0)
+        quantise("g", 1)
+        for h in range(HALVES):
+            multiply("g", 0, h)
+        for h in range(HALVES):
+            c = sb.tile([P, H], U32, name=f"x_codes1{h}", align_bytes=64)
+            nc.vector.tensor_copy(c[:], word_tab[1][:].bitcast(U32).indirect(pieces[h]))
+            x_codes[1, h] = c[:]
+            multiply("g", 1, h)
+        for z in range(PASSES):
+            quantise("y", z)
             for h in range(HALVES):
-                acc[name, h] = ps.tile([P, H], F32, name=f"acc_{name}{h}")
-            for z in range(PASSES):
-                grouped = sb.tile([P, N, PACK], BF16, name=f"grouped_{name}{z}", align_bytes=64)
-                nc.scalar.copy(
-                    grouped[:].rearrange("p (c i) t -> p c t i", i=4),
-                    raw[name, z][:].rearrange("p t (c i) -> p c t i", i=4),
-                )
-                codes = sb.tile([P, N], U32, name=f"w_codes_{name}{z}", align_bytes=64)
-                scales = sb.tile([P, N], U8, name=f"w_scales_{name}{z}", align_bytes=64)
-                nc.vector.quantize_mx(
-                    out=codes[:].bitcast(FP8X4),
-                    scales=scales[:],
-                    in_=grouped[:].rearrange("p m t -> p (m t)"),
-                )
-                for h in range(HALVES):
-                    cols = slice(h * H, (h + 1) * H)
-                    nc.tensor.matmul_mx(
-                        out=acc[name, h][:],
-                        lhsT=codes[:].bitcast(FP8X4),
-                        lhsT_scale=scales[:],
-                        rhs=x_codes[z][:, cols].bitcast(FP8X4),
-                        rhs_scale=x_sc[4 * z : P, cols],
-                        start=(z == 0),
-                        stop=(z == PASSES - 1),
-                    )
+                multiply("y", z, h)
 
         carry, gate, passed, layer = [], [], [], []
         for h in range(HALVES):
             c = sb.tile([P, H], F32, name=f"carry{h}")
             nc.scalar.activation(c[:], acc["g", h][:], ACT.Sigmoid, scale=-1.0)
             carry.append(c)
-        for h in range(HALVES):
             g = sb.tile([P, H], F32, name=f"gate{h}")
             nc.scalar.activation(g[:], acc["g", h][:], ACT.Sigmoid)
             gate.append(g)
         for h in range(HALVES):
             t = sb.tile([P, H], F32, name=f"passed{h}")
-            piece = offsets[:, h * H // LIST_COLS : (h + 1) * H // LIST_COLS]
-            nc.vector.tensor_tensor(t[:], res_tab[:].indirect(piece), carry[h][:], ALU.mult)
+            nc.vector.tensor_tensor(t[:], res_tab[:].indirect(pieces[h]), carry[h][:], ALU.mult)
             passed.append(t)
         for h in range(HALVES):
-            a = sb.tile([P, H], F32, name=f"layer{h}")
+            a = carry[h]
             nc.vector.scalar_tensor_tensor(a[:], acc["y", h][:], 0.0, gate[h][:], ALU.max, ALU.mult)
             layer.append(a)
         for h in range(HALVES):

@@ -31,7 +31,6 @@ def tile_picked_highway_relu_p_kernel(tc, x_words, x_scales, res, w1, w2, offs, 
         ps = ctx.enter_context(tc.psum_pool(name="ps", bufs=1))
 
         offsets = sb.tile([P, S // LIST_COLS], U16, name="offsets")
-        nc.sync.dma_start(offsets[:], offs)
 
         scale_tab = sb.tile([P, T], U8, name="scale_tab", align_bytes=64)
         nc.vector.memset(scale_tab[:].bitcast(I32), 0)
@@ -54,6 +53,7 @@ def tile_picked_highway_relu_p_kernel(tc, x_words, x_scales, res, w1, w2, offs, 
             raw[name, z] = t
 
         load_words(0)
+        nc.sync.dma_start(offsets[:], offs)
         scales_i32 = x_scales.bitcast(I32)
         for q in range(4):
             nc.sync.dma_start(

@@ -21,6 +21,8 @@ K_PASS = P * PACK
 PASSES = K // K_PASS
 HALVES = 2
 H = S // HALVES
+QUARTERS = 4
+Q = S // QUARTERS
 LIST_COLS = 16
 
 
@@ -48,7 +50,7 @@ def tile_picked_highway_relu_p_kernel(tc, x_words, x_scales, res, w1, w2, offs, 
             word_tab[z] = tab
 
         def load_weights(name, w, z):
-            t = sb.tile([P, PACK, N], F32, name=f"raw_{name}{z}", align_bytes=64)
+            t = sb.tile([P, PACK, N], F32, name=f"raw_{name}{z}", tag=f"raw_{name}{z}", align_bytes=64)
             nc.sync.dma_start(t[:], w[z * K_PASS : (z + 1) * K_PASS, :].rearrange("(p j) m -> p j m", j=PACK))
             raw[name, z] = t
 
@@ -69,24 +71,23 @@ def tile_picked_highway_relu_p_kernel(tc, x_words, x_scales, res, w1, w2, offs, 
         res_tab = sb.tile([P, T], F32, name="res_tab", align_bytes=64)
         nc.sync.dma_start(res_tab[:], res)
 
-        pieces = [offsets[:, h * H // LIST_COLS : (h + 1) * H // LIST_COLS] for h in range(HALVES)]
-        x_codes = {}
-        c = sb.tile([P, S], U32, name="x_codes0", align_bytes=64)
-        nc.vector.tensor_copy(c[:], word_tab[0][:].bitcast(U32).indirect(offsets[:]))
-        for h in range(HALVES):
-            x_codes[0, h] = c[:, h * H : (h + 1) * H]
+        quarter = [offsets[:, a * Q // LIST_COLS : (a + 1) * Q // LIST_COLS] for a in range(QUARTERS)]
+        codes0 = sb.tile([P, S], U32, name="x_codes0", align_bytes=64)
+        nc.vector.tensor_copy(codes0[:], word_tab[0][:].bitcast(U32).indirect(offsets[:]))
         x_sc = sb.tile([P, S], U8, name="x_sc", align_bytes=64)
         nc.vector.tensor_copy(x_sc[:], scale_tab[:].indirect(offsets[:]))
+        codes1 = sb.tile([P, S], U32, name="x_codes1", align_bytes=64)
+        x_codes = [codes0, codes1]
 
         w_codes, w_scales = {}, {}
 
-        def quantise(name, z):
-            grouped = sb.tile([P, N, PACK], BF16, name=f"grouped_{name}{z}", align_bytes=64)
-            cast = nc.vector.tensor_copy if (name, z) == ("y", PASSES - 1) else nc.scalar.copy
-            cast(
-                grouped[:].rearrange("p (c i) t -> p c t i", i=4),
-                raw[name, z][:].rearrange("p t (c i) -> p c t i", i=4),
-            )
+        def quantise(name, z, shares):
+            grouped = sb.tile([P, N, PACK], BF16, name=f"grouped_{name}{z}", tag=f"grouped_{name}{z}", align_bytes=64)
+            for cast, lo, hi in shares:
+                cast(
+                    grouped[:, lo:hi, :].rearrange("p (c i) t -> p c t i", i=4),
+                    raw[name, z][:, :, lo:hi].rearrange("p t (c i) -> p c t i", i=4),
+                )
             codes = sb.tile([P, N], U32, name=f"w_codes_{name}{z}", align_bytes=64)
             scales = sb.tile([P, N], U8, name=f"w_scales_{name}{z}", align_bytes=64)
             nc.vector.quantize_mx(
@@ -96,50 +97,50 @@ def tile_picked_highway_relu_p_kernel(tc, x_words, x_scales, res, w1, w2, offs, 
             )
             w_codes[name, z], w_scales[name, z] = codes, scales
 
-        acc = {(name, h): ps.tile([P, H], F32, name=f"acc_{name}{h}") for name in ("g", "y") for h in range(HALVES)}
+        acc_g = [ps.tile([P, Q], F32, name=f"acc_g{a}") for a in range(QUARTERS)]
+        acc_y = [ps.tile([P, H], F32, name=f"acc_y{h}") for h in range(HALVES)]
 
-        def multiply(name, z, h):
+        def multiply(acc, name, z, lo, hi):
             nc.tensor.matmul_mx(
-                out=acc[name, h][:],
+                out=acc[:],
                 lhsT=w_codes[name, z][:].bitcast(FP8X4),
                 lhsT_scale=w_scales[name, z][:],
-                rhs=x_codes[z, h].bitcast(FP8X4),
-                rhs_scale=x_sc[4 * z : P, h * H : (h + 1) * H],
+                rhs=x_codes[z][:, lo:hi].bitcast(FP8X4),
+                rhs_scale=x_sc[4 * z : P, lo:hi],
                 start=(z == 0),
                 stop=(z == PASSES - 1),
             )
 
-        quantise("g", 0)
-        quantise("g", 1)
-        for h in range(HALVES):
-            multiply("g", 0, h)
-        for h in range(HALVES):
-            c = sb.tile([P, H], U32, name=f"x_codes1{h}", align_bytes=64)
-            nc.vector.tensor_copy(c[:], word_tab[1][:].bitcast(U32).indirect(pieces[h]))
-            x_codes[1, h] = c[:]
-            multiply("g", 1, h)
+        on_scalar = [(nc.scalar.copy, 0, N)]
+        quantise("g", 0, on_scalar)
+        quantise("g", 1, on_scalar)
+        for a in range(QUARTERS):
+            multiply(acc_g[a], "g", 0, a * Q, (a + 1) * Q)
+        for a in range(QUARTERS):
+            nc.vector.tensor_copy(codes1[:, a * Q : (a + 1) * Q], word_tab[1][:].bitcast(U32).indirect(quarter[a]))
+            multiply(acc_g[a], "g", 1, a * Q, (a + 1) * Q)
+        quantise("y", 0, on_scalar)
+        quantise("y", 1, [(nc.vector.tensor_copy, 0, N)])
         for z in range(PASSES):
-            quantise("y", z)
             for h in range(HALVES):
-                multiply("y", z, h)
+                multiply(acc_y[h], "y", z, h * H, (h + 1) * H)
 
-        carry, gate, passed, layer = [], [], [], []
+        carry = sb.tile([P, S], F32, name="carry", tag="raw_y0", align_bytes=64)
+        gate = sb.tile([P, S], F32, name="gate", tag="grouped_y0", align_bytes=64)
+        passed = sb.tile([P, S], F32, name="passed")
+        for a in range(QUARTERS):
+            nc.scalar.activation(carry[:, a * Q : (a + 1) * Q], acc_g[a][:], ACT.Sigmoid, scale=-1.0)
+        for a in range(QUARTERS):
+            nc.scalar.activation(gate[:, a * Q : (a + 1) * Q], acc_g[a][:], ACT.Sigmoid)
         for h in range(HALVES):
-            c = sb.tile([P, H], F32, name=f"carry{h}")
-            nc.scalar.activation(c[:], acc["g", h][:], ACT.Sigmoid, scale=-1.0)
-            carry.append(c)
-            g = sb.tile([P, H], F32, name=f"gate{h}")
-            nc.scalar.activation(g[:], acc["g", h][:], ACT.Sigmoid)
-            gate.append(g)
+            cols = slice(h * H, (h + 1) * H)
+            half = offsets[:, h * H // LIST_COLS : (h + 1) * H // LIST_COLS]
+            nc.vector.tensor_tensor(passed[:, cols], res_tab[:].indirect(half), carry[:, cols], ALU.mult)
         for h in range(HALVES):
-            t = sb.tile([P, H], F32, name=f"passed{h}")
-            nc.vector.tensor_tensor(t[:], res_tab[:].indirect(pieces[h]), carry[h][:], ALU.mult)
-            passed.append(t)
+            cols = slice(h * H, (h + 1) * H)
+            nc.vector.scalar_tensor_tensor(carry[:, cols], acc_y[h][:], 0.0, gate[:, cols], ALU.max, ALU.mult)
         for h in range(HALVES):
-            a = carry[h]
-            nc.vector.scalar_tensor_tensor(a[:], acc["y", h][:], 0.0, gate[h][:], ALU.max, ALU.mult)
-            layer.append(a)
-        for h in range(HALVES):
+            cols = slice(h * H, (h + 1) * H)
             o = sb.tile([P, H], F32, name=f"result{h}")
-            nc.vector.tensor_tensor(o[:], layer[h][:], passed[h][:], ALU.add)
-            nc.sync.dma_start(out[:, h * H : (h + 1) * H], o[:])
+            nc.vector.tensor_tensor(o[:], carry[:, cols], passed[:, cols], ALU.add)
+            nc.sync.dma_start(out[:, cols], o[:])

@@ -122,25 +122,26 @@ def tile_picked_highway_relu_p_kernel(tc, x_words, x_scales, res, w1, w2, offs, 
         quantise("y", 0, on_scalar)
         quantise("y", 1, [(nc.vector.tensor_copy, 0, N)])
         for z in range(PASSES):
-            for h in range(HALVES):
+            for h in reversed(range(HALVES)):
                 multiply(acc_y[h], "y", z, h * H, (h + 1) * H)
 
         carry = sb.tile([P, S], F32, name="carry", tag="raw_y0", align_bytes=64)
         gate = sb.tile([P, S], F32, name="gate", tag="grouped_y0", align_bytes=64)
+        picked = sb.tile([P, H], F32, name="picked")
         passed = sb.tile([P, S], F32, name="passed")
-        for a in range(QUARTERS):
-            nc.scalar.activation(carry[:, a * Q : (a + 1) * Q], acc_g[a][:], ACT.Sigmoid, scale=-1.0)
-        for a in range(QUARTERS):
+        first, second = slice(0, H), slice(H, S)
+        spot = [slice(H, H + Q), slice(0, Q)]
+        for a in range(HALVES):
+            nc.scalar.activation(carry[:, spot[a]], acc_g[a][:], ACT.Sigmoid, scale=-1.0)
+        for a in (2, 3, 0, 1):
             nc.scalar.activation(gate[:, a * Q : (a + 1) * Q], acc_g[a][:], ACT.Sigmoid)
-        for h in range(HALVES):
-            cols = slice(h * H, (h + 1) * H)
-            half = offsets[:, h * H // LIST_COLS : (h + 1) * H // LIST_COLS]
-            nc.vector.tensor_tensor(passed[:, cols], res_tab[:].indirect(half), carry[:, cols], ALU.mult)
-        for h in range(HALVES):
-            cols = slice(h * H, (h + 1) * H)
+        nc.scalar.activation(picked[:], res_tab[:].indirect(offsets[:, H // LIST_COLS :]), ACT.Copy)
+        for a in range(HALVES):
+            nc.vector.tensor_tensor(passed[:, a * Q : (a + 1) * Q], res_tab[:].indirect(quarter[a]), carry[:, spot[a]], ALU.mult)
+        for h, cols in ((1, second), (0, first)):
             nc.vector.scalar_tensor_tensor(carry[:, cols], acc_y[h][:], 0.0, gate[:, cols], ALU.max, ALU.mult)
-        for h in range(HALVES):
-            cols = slice(h * H, (h + 1) * H)
-            o = sb.tile([P, H], F32, name=f"result{h}")
-            nc.vector.tensor_tensor(o[:], carry[:, cols], passed[:, cols], ALU.add)
+        nc.vector.scalar_tensor_tensor(passed[:, second], gate[:, second], 1.0, picked[:], ALU.subtract, ALU.mult)
+        for cols, op in ((first, ALU.add), (second, ALU.subtract)):
+            o = sb.tile([P, H], F32, name=f"result{cols.start}")
+            nc.vector.tensor_tensor(o[:], carry[:, cols], passed[:, cols], op)
             nc.sync.dma_start(out[:, cols], o[:])

@@ -67,42 +67,38 @@ def tile_picked_highway_relu_p_kernel(tc, x_words, x_scales, res, w1, w2, offs, 
         load_words(1)
         for z in range(PASSES):
             load_weights("y", w1, z)
-
         res_tab = sb.tile([P, T], F32, name="res_tab", align_bytes=64)
         nc.sync.dma_start(res_tab[:], res)
 
-        quarter = [offsets[:, a * Q // LIST_COLS : (a + 1) * Q // LIST_COLS] for a in range(QUARTERS)]
-        codes0 = sb.tile([P, S], U32, name="x_codes0", align_bytes=64)
-        nc.vector.tensor_copy(codes0[:], word_tab[0][:].bitcast(U32).indirect(offsets[:]))
+        x_codes = [sb.tile([P, S], U32, name=f"x_codes{z}", align_bytes=64) for z in range(PASSES)]
         x_sc = sb.tile([P, S], U8, name="x_sc", align_bytes=64)
+        nc.vector.tensor_copy(x_codes[0][:], word_tab[0][:].bitcast(U32).indirect(offsets[:]))
         nc.vector.tensor_copy(x_sc[:], scale_tab[:].indirect(offsets[:]))
-        codes1 = sb.tile([P, S], U32, name="x_codes1", align_bytes=64)
-        x_codes = [codes0, codes1]
 
-        w_codes, w_scales = {}, {}
+        w_codes, w_scales, grouped = {}, {}, {}
 
-        def quantise(name, z, shares):
-            grouped = sb.tile([P, N, PACK], BF16, name=f"grouped_{name}{z}", tag=f"grouped_{name}{z}", align_bytes=64)
+        def round_weights(name, z, shares):
+            g = sb.tile([P, N, PACK], BF16, name=f"grouped_{name}{z}", tag=f"grouped_{name}{z}", align_bytes=64)
             for cast, lo, hi in shares:
                 cast(
-                    grouped[:, lo:hi, :].rearrange("p (c i) t -> p c t i", i=4),
+                    g[:, lo:hi, :].rearrange("p (c i) t -> p c t i", i=4),
                     raw[name, z][:, :, lo:hi].rearrange("p t (c i) -> p c t i", i=4),
                 )
+            grouped[name, z] = g
+
+        def quantise(name, z):
             codes = sb.tile([P, N], U32, name=f"w_codes_{name}{z}", align_bytes=64)
             scales = sb.tile([P, N], U8, name=f"w_scales_{name}{z}", align_bytes=64)
             nc.vector.quantize_mx(
                 out=codes[:].bitcast(FP8X4),
                 scales=scales[:],
-                in_=grouped[:].rearrange("p m t -> p (m t)"),
+                in_=grouped[name, z][:].rearrange("p m t -> p (m t)"),
             )
             w_codes[name, z], w_scales[name, z] = codes, scales
 
-        acc_g = [ps.tile([P, Q], F32, name=f"acc_g{a}") for a in range(QUARTERS)]
-        acc_y = [ps.tile([P, H], F32, name=f"acc_y{h}") for h in range(HALVES)]
-
         def multiply(acc, name, z, lo, hi):
             nc.tensor.matmul_mx(
-                out=acc[:],
+                out=acc,
                 lhsT=w_codes[name, z][:].bitcast(FP8X4),
                 lhsT_scale=w_scales[name, z][:],
                 rhs=x_codes[z][:, lo:hi].bitcast(FP8X4),
@@ -111,37 +107,46 @@ def tile_picked_highway_relu_p_kernel(tc, x_words, x_scales, res, w1, w2, offs, 
                 stop=(z == PASSES - 1),
             )
 
-        on_scalar = [(nc.scalar.copy, 0, N)]
-        quantise("g", 0, on_scalar)
-        quantise("g", 1, on_scalar)
-        for a in range(QUARTERS):
-            multiply(acc_g[a], "g", 0, a * Q, (a + 1) * Q)
-        for a in range(QUARTERS):
-            nc.vector.tensor_copy(codes1[:, a * Q : (a + 1) * Q], word_tab[1][:].bitcast(U32).indirect(quarter[a]))
-            multiply(acc_g[a], "g", 1, a * Q, (a + 1) * Q)
-        quantise("y", 0, on_scalar)
-        quantise("y", 1, [(nc.vector.tensor_copy, 0, N)])
-        for z in range(PASSES):
-            for h in reversed(range(HALVES)):
-                multiply(acc_y[h], "y", z, h * H, (h + 1) * H)
+        def entries(lo, hi):
+            return offsets[:, lo // LIST_COLS : hi // LIST_COLS]
 
-        carry = sb.tile([P, S], F32, name="carry", tag="raw_y0", align_bytes=64)
-        gate = sb.tile([P, S], F32, name="gate", tag="grouped_y0", align_bytes=64)
+        def negated_on_scalar(dst, src):
+            nc.scalar.activation(dst, src, ACT.Copy, scale=-1.0)
+
+        def negated_on_vector(dst, src):
+            nc.vector.tensor_scalar(dst, src, -1.0, None, ALU.mult)
+
+        acc_g = [ps.tile([P, H], F32, name=f"acc_g{h}") for h in range(HALVES)]
+        acc_y = [ps.tile([P, H], F32, name=f"acc_y{h}") for h in range(HALVES)]
+        halves = [slice(h * H, (h + 1) * H) for h in range(HALVES)]
+        first, second = halves
+
+        for z in range(PASSES):
+            round_weights("g", z, [(nc.scalar.copy, 0, N)])
+            quantise("g", z)
+        for h, cols in enumerate(halves):
+            multiply(acc_g[h][:], "g", 0, cols.start, cols.stop)
+        for h, cols in enumerate(halves):
+            nc.vector.tensor_copy(x_codes[1][:, cols], word_tab[1][:].bitcast(U32).indirect(entries(cols.start, cols.stop)))
+            multiply(acc_g[h][:], "g", 1, cols.start, cols.stop)
+        for z in range(PASSES):
+            round_weights("y", z, [(negated_on_scalar, 0, N)])
+            quantise("y", z)
+            for h in range(HALVES):
+                multiply(acc_y[h][:], "y", z, h * H, (h + 1) * H)
+
+        carry = sb.tile([P, S], F32, name="carry", tag="raw_y1", align_bytes=64)
         picked = sb.tile([P, H], F32, name="picked")
+        gated = sb.tile([P, S], F32, name="gated")
         passed = sb.tile([P, S], F32, name="passed")
-        first, second = slice(0, H), slice(H, S)
-        spot = [slice(H, H + Q), slice(0, Q)]
-        for a in range(HALVES):
-            nc.scalar.activation(carry[:, spot[a]], acc_g[a][:], ACT.Sigmoid, scale=-1.0)
-        for a in (2, 3, 0, 1):
-            nc.scalar.activation(gate[:, a * Q : (a + 1) * Q], acc_g[a][:], ACT.Sigmoid)
-        nc.scalar.activation(picked[:], res_tab[:].indirect(offsets[:, H // LIST_COLS :]), ACT.Copy)
-        for a in range(HALVES):
-            nc.vector.tensor_tensor(passed[:, a * Q : (a + 1) * Q], res_tab[:].indirect(quarter[a]), carry[:, spot[a]], ALU.mult)
-        for h, cols in ((1, second), (0, first)):
-            nc.vector.scalar_tensor_tensor(carry[:, cols], acc_y[h][:], 0.0, gate[:, cols], ALU.max, ALU.mult)
-        nc.vector.scalar_tensor_tensor(passed[:, second], gate[:, second], 1.0, picked[:], ALU.subtract, ALU.mult)
-        for cols, op in ((first, ALU.add), (second, ALU.subtract)):
+        for h, cols in enumerate(halves):
+            nc.scalar.activation(carry[:, cols], acc_g[h][:], ACT.Sigmoid, scale=-1.0)
+        nc.scalar.activation(picked[:], res_tab[:].indirect(entries(H, S)), ACT.Copy)
+        nc.vector.tensor_tensor(passed[:, first], res_tab[:].indirect(entries(0, H)), carry[:, first], ALU.mult)
+        nc.vector.scalar_tensor_tensor(gated[:, first], carry[:, first], 1.0, acc_y[0][:], ALU.subtract, ALU.mult)
+        nc.vector.tensor_tensor(passed[:, second], picked[:], carry[:, second], ALU.mult)
+        nc.vector.scalar_tensor_tensor(gated[:, second], carry[:, second], 1.0, acc_y[1][:], ALU.subtract, ALU.mult)
+        for cols in halves:
             o = sb.tile([P, H], F32, name=f"result{cols.start}")
-            nc.vector.tensor_tensor(o[:], carry[:, cols], passed[:, cols], op)
+            nc.vector.scalar_tensor_tensor(o[:], gated[:, cols], 0.0, passed[:, cols], ALU.max, ALU.add)
             nc.sync.dma_start(out[:, cols], o[:])

@@ -130,19 +130,23 @@ def tile_picked_highway_relu_p_kernel(tc, x_words, x_scales, res, w1, w2, offs, 
             nc.vector.tensor_copy(x_codes[1][:, cols], word_tab[1][:].bitcast(U32).indirect(entries(cols.start, cols.stop)))
             multiply(acc_g[h][:], "g", 1, cols.start, cols.stop)
         for z in range(PASSES):
-            round_weights("y", z, [(negated_on_scalar, 0, N)])
+            round_weights("y", z, [(negated_on_scalar, 0, N)] if z == 0 else [(negated_on_scalar, 0, 80), (negated_on_vector, 80, N)])
             quantise("y", z)
             for h in range(HALVES):
                 multiply(acc_y[h][:], "y", z, h * H, (h + 1) * H)
 
         carry = sb.tile([P, S], F32, name="carry", tag="raw_y1", align_bytes=64)
         picked = sb.tile([P, H], F32, name="picked")
-        gated = sb.tile([P, S], F32, name="gated")
+        gated = sb.tile([P, S], F32, name="gated", tag="raw_y0", align_bytes=64)
         passed = sb.tile([P, S], F32, name="passed")
-        for h, cols in enumerate(halves):
-            nc.scalar.activation(carry[:, cols], acc_g[h][:], ACT.Sigmoid, scale=-1.0)
+        lead = 64
+        lead_carry = gated[:, H - lead // 2 : H + lead // 2]
+        nc.scalar.activation(carry[:, first], acc_g[0][:], ACT.Sigmoid, scale=-1.0)
+        nc.scalar.activation(lead_carry, acc_g[0][:, :lead], ACT.Sigmoid, scale=-1.0)
+        nc.scalar.activation(carry[:, second], acc_g[1][:], ACT.Sigmoid, scale=-1.0)
         nc.scalar.activation(picked[:], res_tab[:].indirect(entries(H, S)), ACT.Copy)
-        nc.vector.tensor_tensor(passed[:, first], res_tab[:].indirect(entries(0, H)), carry[:, first], ALU.mult)
+        nc.vector.tensor_tensor(passed[:, :lead], res_tab[:].indirect(entries(0, lead)), lead_carry, ALU.mult)
+        nc.vector.tensor_tensor(passed[:, lead:H], res_tab[:].indirect(entries(lead, H)), carry[:, lead:H], ALU.mult)
         nc.vector.scalar_tensor_tensor(gated[:, first], carry[:, first], 1.0, acc_y[0][:], ALU.subtract, ALU.mult)
         nc.vector.tensor_tensor(passed[:, second], picked[:], carry[:, second], ALU.mult)
         nc.vector.scalar_tensor_tensor(gated[:, second], carry[:, second], 1.0, acc_y[1][:], ALU.subtract, ALU.mult)

@@ -136,20 +136,22 @@ def tile_picked_highway_relu_p_kernel(tc, x_words, x_scales, res, w1, w2, offs, 
                 multiply(acc_y[h][:], "y", z, h * H, (h + 1) * H)
 
         carry = sb.tile([P, S], F32, name="carry", tag="raw_y1", align_bytes=64)
-        picked = sb.tile([P, H], F32, name="picked")
+        picked = sb.tile([P, S], F32, name="picked")
         gated = sb.tile([P, S], F32, name="gated", tag="raw_y0", align_bytes=64)
         passed = sb.tile([P, S], F32, name="passed")
-        lead = 64
-        lead_carry = gated[:, H - lead // 2 : H + lead // 2]
+        lead, fused, on_gpsimd, on_vector = slice(0, 64), slice(64, 192), slice(192, 320), slice(320, S)
+        lead_carry = gated[:, H - lead.stop // 2 : H + lead.stop // 2]
         nc.scalar.activation(carry[:, first], acc_g[0][:], ACT.Sigmoid, scale=-1.0)
-        nc.scalar.activation(lead_carry, acc_g[0][:, :lead], ACT.Sigmoid, scale=-1.0)
+        nc.scalar.activation(lead_carry, acc_g[0][:, lead], ACT.Sigmoid, scale=-1.0)
         nc.scalar.activation(carry[:, second], acc_g[1][:], ACT.Sigmoid, scale=-1.0)
-        nc.scalar.activation(picked[:], res_tab[:].indirect(entries(H, S)), ACT.Copy)
-        nc.vector.tensor_tensor(passed[:, :lead], res_tab[:].indirect(entries(0, lead)), lead_carry, ALU.mult)
-        nc.vector.tensor_tensor(passed[:, lead:H], res_tab[:].indirect(entries(lead, H)), carry[:, lead:H], ALU.mult)
-        nc.vector.scalar_tensor_tensor(gated[:, first], carry[:, first], 1.0, acc_y[0][:], ALU.subtract, ALU.mult)
-        nc.vector.tensor_tensor(passed[:, second], picked[:], carry[:, second], ALU.mult)
-        nc.vector.scalar_tensor_tensor(gated[:, second], carry[:, second], 1.0, acc_y[1][:], ALU.subtract, ALU.mult)
+        for cols in (on_gpsimd, on_vector):
+            nc.scalar.activation(picked[:, cols], res_tab[:].indirect(entries(cols.start, cols.stop)), ACT.Copy)
+        nc.vector.tensor_tensor(passed[:, lead], res_tab[:].indirect(entries(lead.start, lead.stop)), lead_carry, ALU.mult)
+        nc.vector.tensor_tensor(passed[:, fused], res_tab[:].indirect(entries(fused.start, fused.stop)), carry[:, fused], ALU.mult)
+        nc.gpsimd.tensor_tensor(passed[:, on_gpsimd], picked[:, on_gpsimd], carry[:, on_gpsimd], ALU.mult)
+        for h, cols in enumerate(halves):
+            nc.vector.scalar_tensor_tensor(gated[:, cols], carry[:, cols], 1.0, acc_y[h][:], ALU.subtract, ALU.mult)
+        nc.vector.tensor_tensor(passed[:, on_vector], picked[:, on_vector], carry[:, on_vector], ALU.mult)
         for cols in halves:
             o = sb.tile([P, H], F32, name=f"result{cols.start}")
             nc.vector.scalar_tensor_tensor(o[:], gated[:, cols], 0.0, passed[:, cols], ALU.max, ALU.add)

@@ -54,7 +54,7 @@ def tile_picked_highway_relu_p_kernel(tc, x_words, x_scales, res, w1, w2, offs, 
             nc.sync.dma_start(t[:], w[z * K_PASS : (z + 1) * K_PASS, :].rearrange("(p j) m -> p j m", j=PACK))
             raw[name, z] = t
 
-        load_words(0)
+        load_weights("g", w2, 0)
         nc.sync.dma_start(offsets[:], offs)
         scales_i32 = x_scales.bitcast(I32)
         for q in range(4):
@@ -62,7 +62,7 @@ def tile_picked_highway_relu_p_kernel(tc, x_words, x_scales, res, w1, w2, offs, 
                 scale_tab[32 * q : 32 * q + 4 * PASSES, :].bitcast(I32),
                 scales_i32[:, 4 * q : 4 * q + 4, :],
             )
-        load_weights("g", w2, 0)
+        load_words(0)
         load_weights("g", w2, 1)
         load_words(1)
         for z in range(PASSES):
@@ -72,8 +72,6 @@ def tile_picked_highway_relu_p_kernel(tc, x_words, x_scales, res, w1, w2, offs, 
 
         x_codes = [sb.tile([P, S], U32, name=f"x_codes{z}", align_bytes=64) for z in range(PASSES)]
         x_sc = sb.tile([P, S], U8, name="x_sc", align_bytes=64)
-        nc.vector.tensor_copy(x_codes[0][:], word_tab[0][:].bitcast(U32).indirect(offsets[:]))
-        nc.vector.tensor_copy(x_sc[:], scale_tab[:].indirect(offsets[:]))
 
         w_codes, w_scales, grouped = {}, {}, {}
 
@@ -121,11 +119,14 @@ def tile_picked_highway_relu_p_kernel(tc, x_words, x_scales, res, w1, w2, offs, 
         halves = [slice(h * H, (h + 1) * H) for h in range(HALVES)]
         first, second = halves
 
-        for z in range(PASSES):
-            round_weights("g", z, [(nc.scalar.copy, 0, N)])
-            quantise("g", z)
+        round_weights("g", 0, [(nc.vector.tensor_copy, 0, N)])
+        quantise("g", 0)
+        nc.vector.tensor_copy(x_sc[:], scale_tab[:].indirect(offsets[:]))
+        nc.vector.tensor_copy(x_codes[0][:], word_tab[0][:].bitcast(U32).indirect(offsets[:]))
         for h, cols in enumerate(halves):
             multiply(acc_g[h][:], "g", 0, cols.start, cols.stop)
+        round_weights("g", 1, [(nc.scalar.copy, 0, N)])
+        quantise("g", 1)
         for h, cols in enumerate(halves):
             nc.vector.tensor_copy(x_codes[1][:, cols], word_tab[1][:].bitcast(U32).indirect(entries(cols.start, cols.stop)))
             multiply(acc_g[h][:], "g", 1, cols.start, cols.stop)

@@ -94,7 +94,7 @@ def tile_picked_highway_relu_p_kernel(tc, x_words, x_scales, res, w1, w2, offs, 
             )
             w_codes[name, z], w_scales[name, z] = codes, scales
 
-        def multiply(acc, name, z, lo, hi):
+        def multiply(acc, name, z, lo, hi, closes=True):
             nc.tensor.matmul_mx(
                 out=acc,
                 lhsT=w_codes[name, z][:].bitcast(FP8X4),
@@ -102,7 +102,7 @@ def tile_picked_highway_relu_p_kernel(tc, x_words, x_scales, res, w1, w2, offs, 
                 rhs=x_codes[z][:, lo:hi].bitcast(FP8X4),
                 rhs_scale=x_sc[4 * z : P, lo:hi],
                 start=(z == 0),
-                stop=(z == PASSES - 1),
+                stop=(z == PASSES - 1 and closes),
             )
 
         def entries(lo, hi):
@@ -127,11 +127,11 @@ def tile_picked_highway_relu_p_kernel(tc, x_words, x_scales, res, w1, w2, offs, 
             multiply(acc_g[h][:], "g", 0, cols.start, cols.stop)
         round_weights("g", 1, [(nc.scalar.copy, 0, N)])
         quantise("g", 1)
-        for h, cols in enumerate(halves):
-            nc.vector.tensor_copy(x_codes[1][:, cols], word_tab[1][:].bitcast(U32).indirect(entries(cols.start, cols.stop)))
-            multiply(acc_g[h][:], "g", 1, cols.start, cols.stop)
+        for lo, hi in ((0, H), (H, H + Q), (H + Q, S)):
+            nc.vector.tensor_copy(x_codes[1][:, lo:hi], word_tab[1][:].bitcast(U32).indirect(entries(lo, hi)))
+            multiply(acc_g[lo // H][:, lo % H : lo % H + hi - lo], "g", 1, lo, hi, closes=(hi % H == 0))
         for z in range(PASSES):
-            round_weights("y", z, [(negated_on_scalar, 0, N)] if z == 0 else [(negated_on_scalar, 0, 80), (negated_on_vector, 80, N)])
+            round_weights("y", z, [(negated_on_scalar, 0, N)] if z == 0 else [(negated_on_scalar, 0, 64), (negated_on_vector, 64, N)])
             quantise("y", z)
             for h in range(HALVES):
                 multiply(acc_y[h][:], "y", z, h * H, (h + 1) * H)

@@ -140,10 +140,10 @@ def tile_picked_highway_relu_p_kernel(tc, x_words, x_scales, res, w1, w2, offs, 
         picked = sb.tile([P, S], F32, name="picked")
         gated = sb.tile([P, S], F32, name="gated", tag="raw_y0", align_bytes=64)
         passed = sb.tile([P, S], F32, name="passed")
-        lead, fused, on_gpsimd, on_vector = slice(0, 64), slice(64, 192), slice(192, 320), slice(320, S)
+        lead, fused, on_gpsimd, on_vector = slice(0, 64), slice(64, H), slice(H, H + Q), slice(H + Q, S)
         lead_carry = gated[:, H - lead.stop // 2 : H + lead.stop // 2]
-        nc.scalar.activation(carry[:, first], acc_g[0][:], ACT.Sigmoid, scale=-1.0)
         nc.scalar.activation(lead_carry, acc_g[0][:, lead], ACT.Sigmoid, scale=-1.0)
+        nc.scalar.activation(carry[:, first], acc_g[0][:], ACT.Sigmoid, scale=-1.0)
         nc.scalar.activation(carry[:, second], acc_g[1][:], ACT.Sigmoid, scale=-1.0)
         for cols in (on_gpsimd, on_vector):
             nc.scalar.activation(picked[:, cols], res_tab[:].indirect(entries(cols.start, cols.stop)), ACT.Copy)

@@ -140,19 +140,20 @@ def tile_picked_highway_relu_p_kernel(tc, x_words, x_scales, res, w1, w2, offs, 
         picked = sb.tile([P, S], F32, name="picked")
         gated = sb.tile([P, S], F32, name="gated", tag="raw_y0", align_bytes=64)
         passed = sb.tile([P, S], F32, name="passed")
-        lead, fused, on_gpsimd, on_vector = slice(0, 64), slice(64, H), slice(H, H + Q), slice(H + Q, S)
+        lead, fused = slice(0, 64), slice(64, H)
+        on_gpsimd = [slice(H, H + Q), slice(H + Q, S)]
         lead_carry = gated[:, H - lead.stop // 2 : H + lead.stop // 2]
         nc.scalar.activation(lead_carry, acc_g[0][:, lead], ACT.Sigmoid, scale=-1.0)
         nc.scalar.activation(carry[:, first], acc_g[0][:], ACT.Sigmoid, scale=-1.0)
         nc.scalar.activation(carry[:, second], acc_g[1][:], ACT.Sigmoid, scale=-1.0)
-        for cols in (on_gpsimd, on_vector):
+        for cols in on_gpsimd:
             nc.scalar.activation(picked[:, cols], res_tab[:].indirect(entries(cols.start, cols.stop)), ACT.Copy)
         nc.vector.tensor_tensor(passed[:, lead], res_tab[:].indirect(entries(lead.start, lead.stop)), lead_carry, ALU.mult)
         nc.vector.tensor_tensor(passed[:, fused], res_tab[:].indirect(entries(fused.start, fused.stop)), carry[:, fused], ALU.mult)
-        nc.gpsimd.tensor_tensor(passed[:, on_gpsimd], picked[:, on_gpsimd], carry[:, on_gpsimd], ALU.mult)
+        for cols in on_gpsimd:
+            nc.gpsimd.tensor_tensor(passed[:, cols], picked[:, cols], carry[:, cols], ALU.mult)
         for h, cols in enumerate(halves):
             nc.vector.scalar_tensor_tensor(gated[:, cols], carry[:, cols], 1.0, acc_y[h][:], ALU.subtract, ALU.mult)
-        nc.vector.tensor_tensor(passed[:, on_vector], picked[:, on_vector], carry[:, on_vector], ALU.mult)
         for cols in halves:
             o = sb.tile([P, H], F32, name=f"result{cols.start}")
             nc.vector.scalar_tensor_tensor(o[:], gated[:, cols], 0.0, passed[:, cols], ALU.max, ALU.add)

@@ -41,6 +41,8 @@ def tile_picked_highway_relu_p_kernel(tc, x_words, x_scales, res, w1, w2, offs, 
         warm_out = sb.tile([P, 8], F32, name="warm_out")
         nc.vector.memset(warm_in[:], 0.0)
         nc.scalar.activation(warm_out[:], warm_in[:], ACT.Sigmoid)
+        warm_product = sb.tile([P, 8], F32, name="warm_product")
+        nc.gpsimd.tensor_tensor(warm_product[:], warm_in[:], warm_in[:], ALU.mult)
 
         word_tab, raw = {}, {}
 

@@ -24,6 +24,7 @@ H = S // HALVES
 QUARTERS = 4
 Q = S // QUARTERS
 LIST_COLS = 16
+ALIGN = 256
 
 
 def tile_picked_highway_relu_p_kernel(tc, x_words, x_scales, res, w1, w2, offs, out):
@@ -34,7 +35,7 @@ def tile_picked_highway_relu_p_kernel(tc, x_words, x_scales, res, w1, w2, offs, 
 
         offsets = sb.tile([P, S // LIST_COLS], U16, name="offsets")
 
-        scale_tab = sb.tile([P, T], U8, name="scale_tab", align_bytes=64)
+        scale_tab = sb.tile([P, T], U8, name="scale_tab", align_bytes=ALIGN)
         nc.vector.memset(scale_tab[:].bitcast(I32), 0)
 
         warm_in = sb.tile([P, 8], F32, name="warm_in")
@@ -47,12 +48,12 @@ def tile_picked_highway_relu_p_kernel(tc, x_words, x_scales, res, w1, w2, offs, 
         word_tab, raw = {}, {}
 
         def load_words(z):
-            tab = sb.tile([P, T], I32, name=f"word_tab{z}", align_bytes=64)
+            tab = sb.tile([P, T], I32, name=f"word_tab{z}", align_bytes=ALIGN)
             nc.sync.dma_start(tab[:], x_words[z].rearrange("p c r -> p (c r)").bitcast(I32))
             word_tab[z] = tab
 
         def load_weights(name, w, z):
-            t = sb.tile([P, PACK, N], F32, name=f"raw_{name}{z}", tag=f"raw_{name}{z}", align_bytes=64)
+            t = sb.tile([P, PACK, N], F32, name=f"raw_{name}{z}", tag=f"raw_{name}{z}", align_bytes=ALIGN)
             nc.sync.dma_start(t[:], w[z * K_PASS : (z + 1) * K_PASS, :].rearrange("(p j) m -> p j m", j=PACK))
             raw[name, z] = t
 
@@ -69,16 +70,16 @@ def tile_picked_highway_relu_p_kernel(tc, x_words, x_scales, res, w1, w2, offs, 
         load_words(1)
         for z in range(PASSES):
             load_weights("y", w1, z)
-        res_tab = sb.tile([P, T], F32, name="res_tab", align_bytes=64)
+        res_tab = sb.tile([P, T], F32, name="res_tab", align_bytes=ALIGN)
         nc.sync.dma_start(res_tab[:], res)
 
-        x_codes = [sb.tile([P, S], U32, name=f"x_codes{z}", align_bytes=64) for z in range(PASSES)]
-        x_sc = sb.tile([P, S], U8, name="x_sc", align_bytes=64)
+        x_codes = [sb.tile([P, S], U32, name=f"x_codes{z}", align_bytes=ALIGN) for z in range(PASSES)]
+        x_sc = sb.tile([P, S], U8, name="x_sc", align_bytes=ALIGN)
 
         w_codes, w_scales, grouped = {}, {}, {}
 
         def round_weights(name, z, shares):
-            g = sb.tile([P, N, PACK], BF16, name=f"grouped_{name}{z}", tag=f"grouped_{name}{z}", align_bytes=64)
+            g = sb.tile([P, N, PACK], BF16, name=f"grouped_{name}{z}", tag=f"grouped_{name}{z}", align_bytes=ALIGN)
             for cast, lo, hi in shares:
                 cast(
                     g[:, lo:hi, :].rearrange("p (c i) t -> p c t i", i=4),
@@ -87,8 +88,8 @@ def tile_picked_highway_relu_p_kernel(tc, x_words, x_scales, res, w1, w2, offs, 
             grouped[name, z] = g
 
         def quantise(name, z):
-            codes = sb.tile([P, N], U32, name=f"w_codes_{name}{z}", align_bytes=64)
-            scales = sb.tile([P, N], U8, name=f"w_scales_{name}{z}", align_bytes=64)
+            codes = sb.tile([P, N], U32, name=f"w_codes_{name}{z}", align_bytes=ALIGN)
+            scales = sb.tile([P, N], U8, name=f"w_scales_{name}{z}", align_bytes=ALIGN)
             nc.vector.quantize_mx(
                 out=codes[:].bitcast(FP8X4),
                 scales=scales[:],
@@ -138,10 +139,10 @@ def tile_picked_highway_relu_p_kernel(tc, x_words, x_scales, res, w1, w2, offs, 
             for h in range(HALVES):
                 multiply(acc_y[h][:], "y", z, h * H, (h + 1) * H)
 
-        carry = sb.tile([P, S], F32, name="carry", tag="raw_y1", align_bytes=64)
-        picked = sb.tile([P, S], F32, name="picked")
-        gated = sb.tile([P, S], F32, name="gated", tag="raw_y0", align_bytes=64)
-        passed = sb.tile([P, S], F32, name="passed")
+        carry = sb.tile([P, S], F32, name="carry", tag="raw_y1", align_bytes=ALIGN)
+        picked = sb.tile([P, S], F32, name="picked", align_bytes=ALIGN)
+        gated = sb.tile([P, S], F32, name="gated", tag="raw_y0", align_bytes=ALIGN)
+        passed = sb.tile([P, S], F32, name="passed", align_bytes=ALIGN)
         lead, fused = slice(0, 64), slice(64, H)
         on_gpsimd = [slice(H, H + Q), slice(H + Q, S)]
         lead_carry = gated[:, H - lead.stop // 2 : H + lead.stop // 2]
@@ -157,6 +158,6 @@ def tile_picked_highway_relu_p_kernel(tc, x_words, x_scales, res, w1, w2, offs, 
         for h, cols in enumerate(halves):
             nc.vector.scalar_tensor_tensor(gated[:, cols], carry[:, cols], 1.0, acc_y[h][:], ALU.subtract, ALU.mult)
         for cols in halves:
-            o = sb.tile([P, H], F32, name=f"result{cols.start}")
+            o = sb.tile([P, H], F32, name=f"result{cols.start}", align_bytes=ALIGN)
             nc.vector.scalar_tensor_tensor(o[:], gated[:, cols], 0.0, passed[:, cols], ALU.max, ALU.add)
             nc.sync.dma_start(out[:, cols], o[:])

@@ -42,8 +42,6 @@ def tile_picked_highway_relu_p_kernel(tc, x_words, x_scales, res, w1, w2, offs, 
         warm_out = sb.tile([P, 8], F32, name="warm_out")
         nc.vector.memset(warm_in[:], 0.0)
         nc.scalar.activation(warm_out[:], warm_in[:], ACT.Sigmoid)
-        warm_product = sb.tile([P, 8], F32, name="warm_product")
-        nc.gpsimd.tensor_tensor(warm_product[:], warm_in[:], warm_in[:], ALU.mult)
 
         word_tab, raw = {}, {}
 

@@ -25,6 +25,7 @@ QUARTERS = 4
 Q = S // QUARTERS
 LIST_COLS = 16
 ALIGN = 256
+RAW_ROW = 4 * PACK * N
 
 
 def tile_picked_highway_relu_p_kernel(tc, x_words, x_scales, res, w1, w2, offs, out):
@@ -35,7 +36,7 @@ def tile_picked_highway_relu_p_kernel(tc, x_words, x_scales, res, w1, w2, offs, 
 
         offsets = sb.tile([P, S // LIST_COLS], U16, name="offsets")
 
-        scale_tab = sb.tile([P, T], U8, name="scale_tab", align_bytes=ALIGN)
+        scale_tab = sb.tile([P, T], U8, name="scale_tab", align_bytes=T)
         nc.vector.memset(scale_tab[:].bitcast(I32), 0)
 
         warm_in = sb.tile([P, 8], F32, name="warm_in")
@@ -46,12 +47,12 @@ def tile_picked_highway_relu_p_kernel(tc, x_words, x_scales, res, w1, w2, offs, 
         word_tab, raw = {}, {}
 
         def load_words(z):
-            tab = sb.tile([P, T], I32, name=f"word_tab{z}", align_bytes=ALIGN)
+            tab = sb.tile([P, T], I32, name=f"word_tab{z}", align_bytes=4 * T)
             nc.sync.dma_start(tab[:], x_words[z].rearrange("p c r -> p (c r)").bitcast(I32))
             word_tab[z] = tab
 
         def load_weights(name, w, z):
-            t = sb.tile([P, PACK, N], F32, name=f"raw_{name}{z}", tag=f"raw_{name}{z}", align_bytes=ALIGN)
+            t = sb.tile([P, PACK, N], F32, name=f"raw_{name}{z}", tag=f"raw_{name}{z}", align_bytes=RAW_ROW)
             nc.sync.dma_start(t[:], w[z * K_PASS : (z + 1) * K_PASS, :].rearrange("(p j) m -> p j m", j=PACK))
             raw[name, z] = t
 
@@ -68,7 +69,7 @@ def tile_picked_highway_relu_p_kernel(tc, x_words, x_scales, res, w1, w2, offs, 
         load_words(1)
         for z in range(PASSES):
             load_weights("y", w1, z)
-        res_tab = sb.tile([P, T], F32, name="res_tab", align_bytes=ALIGN)
+        res_tab = sb.tile([P, T], F32, name="res_tab", align_bytes=4 * T)
         nc.sync.dma_start(res_tab[:], res)
 
         x_codes = [sb.tile([P, S], U32, name=f"x_codes{z}", align_bytes=ALIGN) for z in range(PASSES)]
@@ -137,9 +138,9 @@ def tile_picked_highway_relu_p_kernel(tc, x_words, x_scales, res, w1, w2, offs, 
             for h in range(HALVES):
                 multiply(acc_y[h][:], "y", z, h * H, (h + 1) * H)
 
-        carry = sb.tile([P, S], F32, name="carry", tag="raw_y1", align_bytes=ALIGN)
+        carry = sb.tile([P, S], F32, name="carry", tag="raw_y1", align_bytes=RAW_ROW)
         picked = sb.tile([P, S], F32, name="picked", align_bytes=ALIGN)
-        gated = sb.tile([P, S], F32, name="gated", tag="raw_y0", align_bytes=ALIGN)
+        gated = sb.tile([P, S], F32, name="gated", tag="raw_y0", align_bytes=RAW_ROW)
         passed = sb.tile([P, S], F32, name="passed", align_bytes=ALIGN)
         lead, fused = slice(0, 64), slice(64, H)
         on_gpsimd = [slice(H, H + Q), slice(H + Q, S)]
@@ -156,6 +157,6 @@ def tile_picked_highway_relu_p_kernel(tc, x_words, x_scales, res, w1, w2, offs, 
         for h, cols in enumerate(halves):
             nc.vector.scalar_tensor_tensor(gated[:, cols], carry[:, cols], 1.0, acc_y[h][:], ALU.subtract, ALU.mult)
         for cols in halves:
-            o = sb.tile([P, H], F32, name=f"result{cols.start}", align_bytes=ALIGN)
+            o = sb.tile([P, H], F32, name=f"result{cols.start}", align_bytes=4 * H)
             nc.vector.scalar_tensor_tensor(o[:], gated[:, cols], 0.0, passed[:, cols], ALU.max, ALU.add)
             nc.sync.dma_start(out[:, cols], o[:])

@@ -21,11 +21,12 @@ K_PASS = P * PACK
 PASSES = K // K_PASS
 HALVES = 2
 H = S // HALVES
-QUARTERS = 4
-Q = S // QUARTERS
+Q = S // 4
 LIST_COLS = 16
 ALIGN = 256
 RAW_ROW = 4 * PACK * N
+LEAD = 64
+ON_SCALAR = 64
 
 
 def tile_picked_highway_relu_p_kernel(tc, x_words, x_scales, res, w1, w2, offs, out):
@@ -72,13 +73,11 @@ def tile_picked_highway_relu_p_kernel(tc, x_words, x_scales, res, w1, w2, offs, 
         res_tab = sb.tile([P, T], F32, name="res_tab", align_bytes=4 * T)
         nc.sync.dma_start(res_tab[:], res)
 
-        x_codes = [sb.tile([P, S], U32, name=f"x_codes{z}", align_bytes=ALIGN) for z in range(PASSES)]
         x_sc = sb.tile([P, S], U8, name="x_sc", align_bytes=ALIGN)
-
         w_codes, w_scales, grouped = {}, {}, {}
 
         def round_weights(name, z, shares):
-            g = sb.tile([P, N, PACK], BF16, name=f"grouped_{name}{z}", tag=f"grouped_{name}{z}", align_bytes=ALIGN)
+            g = sb.tile([P, N, PACK], BF16, name=f"grouped_{name}{z}", align_bytes=ALIGN)
             for cast, lo, hi in shares:
                 cast(
                     g[:, lo:hi, :].rearrange("p (c i) t -> p c t i", i=4),
@@ -96,66 +95,82 @@ def tile_picked_highway_relu_p_kernel(tc, x_words, x_scales, res, w1, w2, offs, 
             )
             w_codes[name, z], w_scales[name, z] = codes, scales
 
-        def multiply(acc, name, z, lo, hi, closes=True):
+        def entries(cols):
+            return offsets[:, cols.start // LIST_COLS : cols.stop // LIST_COLS]
+
+        def gather_words(codes, z, cols):
+            nc.vector.tensor_copy(codes, word_tab[z][:].bitcast(U32).indirect(entries(cols)))
+
+        def multiply(acc, name, z, codes, cols, closes=True):
             nc.tensor.matmul_mx(
                 out=acc,
                 lhsT=w_codes[name, z][:].bitcast(FP8X4),
                 lhsT_scale=w_scales[name, z][:],
-                rhs=x_codes[z][:, lo:hi].bitcast(FP8X4),
-                rhs_scale=x_sc[4 * z : P, lo:hi],
+                rhs=codes.bitcast(FP8X4),
+                rhs_scale=x_sc[4 * z : P, cols],
                 start=(z == 0),
                 stop=(z == PASSES - 1 and closes),
             )
 
-        def entries(lo, hi):
-            return offsets[:, lo // LIST_COLS : hi // LIST_COLS]
-
         def negated_on_scalar(dst, src):
             nc.scalar.activation(dst, src, ACT.Copy, scale=-1.0)
 
-        def negated_on_vector(dst, src):
-            nc.vector.tensor_scalar(dst, src, -1.0, None, ALU.mult)
+        def negated_on_gpsimd(dst, src):
+            nc.gpsimd.tensor_scalar(dst, src, -1.0, 0.0, ALU.mult, ALU.add)
 
         acc_g = [ps.tile([P, H], F32, name=f"acc_g{h}") for h in range(HALVES)]
         acc_y = [ps.tile([P, H], F32, name=f"acc_y{h}") for h in range(HALVES)]
         halves = [slice(h * H, (h + 1) * H) for h in range(HALVES)]
+        quarters = [slice(q * Q, (q + 1) * Q) for q in range(4)]
         first, second = halves
+        shared = [(negated_on_scalar, 0, ON_SCALAR), (negated_on_gpsimd, ON_SCALAR, N)]
+
+        codes0 = sb.tile([P, S], U32, name="codes0", align_bytes=ALIGN)
+        codes1 = sb.tile([P, 3 * Q], U32, name="codes1", align_bytes=ALIGN)
 
         round_weights("g", 0, [(nc.vector.tensor_copy, 0, N)])
         quantise("g", 0)
         nc.vector.tensor_copy(x_sc[:], scale_tab[:].indirect(offsets[:]))
-        nc.vector.tensor_copy(x_codes[0][:], word_tab[0][:].bitcast(U32).indirect(offsets[:]))
+        gather_words(codes0[:], 0, slice(0, S))
         for h, cols in enumerate(halves):
-            multiply(acc_g[h][:], "g", 0, cols.start, cols.stop)
+            multiply(acc_g[h][:], "g", 0, codes0[:, cols], cols)
         round_weights("g", 1, [(nc.scalar.copy, 0, N)])
         quantise("g", 1)
-        for lo, hi in ((0, H), (H, H + Q), (H + Q, S)):
-            nc.vector.tensor_copy(x_codes[1][:, lo:hi], word_tab[1][:].bitcast(U32).indirect(entries(lo, hi)))
-            multiply(acc_g[lo // H][:, lo % H : lo % H + hi - lo], "g", 1, lo, hi, closes=(hi % H == 0))
-        for z in range(PASSES):
-            round_weights("y", z, [(negated_on_scalar, 0, N)] if z == 0 else [(negated_on_scalar, 0, 64), (negated_on_vector, 64, N)])
-            quantise("y", z)
-            for h in range(HALVES):
-                multiply(acc_y[h][:], "y", z, h * H, (h + 1) * H)
+        gather_words(codes1[:, first], 1, first)
+        multiply(acc_g[0][:], "g", 1, codes1[:, first], first)
+        gather_words(codes1[:, quarters[2]], 1, quarters[2])
+        multiply(acc_g[1][:, :Q], "g", 1, codes1[:, quarters[2]], quarters[2], closes=False)
+        round_weights("y", 0, shared)
+        quantise("y", 0)
+        multiply(acc_y[0][:], "y", 0, codes0[:, first], first)
+        codes1_last = sb.tile([P, Q], U32, name="codes1_last", tag="raw_y0", align_bytes=RAW_ROW)
+        gather_words(codes1_last[:], 1, quarters[3])
+        multiply(acc_g[1][:, Q:], "g", 1, codes1_last[:], quarters[3])
+        multiply(acc_y[1][:], "y", 0, codes0[:, second], second)
+        round_weights("y", 1, shared)
+        quantise("y", 1)
+        multiply(acc_y[0][:], "y", 1, codes1[:, first], first)
+        multiply(acc_y[1][:, :Q], "y", 1, codes1[:, quarters[2]], quarters[2], closes=False)
+        multiply(acc_y[1][:, Q:], "y", 1, codes1_last[:], quarters[3])
 
-        carry = sb.tile([P, S], F32, name="carry", tag="raw_y1", align_bytes=RAW_ROW)
+        late = sb.tile([P, 2 * S], F32, name="late", tag="raw_y1", align_bytes=RAW_ROW)
+        carry, gated = late[:, :S], late[:, S:]
         picked = sb.tile([P, S], F32, name="picked", align_bytes=ALIGN)
-        gated = sb.tile([P, S], F32, name="gated", tag="raw_y0", align_bytes=RAW_ROW)
         passed = sb.tile([P, S], F32, name="passed", align_bytes=ALIGN)
-        lead, fused = slice(0, 64), slice(64, H)
-        on_gpsimd = [slice(H, H + Q), slice(H + Q, S)]
-        lead_carry = gated[:, H - lead.stop // 2 : H + lead.stop // 2]
+        lead, fused = slice(0, LEAD), slice(LEAD, Q)
+        lead_carry = gated[:, H - LEAD // 2 : H + LEAD // 2]
         nc.scalar.activation(lead_carry, acc_g[0][:, lead], ACT.Sigmoid, scale=-1.0)
         nc.scalar.activation(carry[:, first], acc_g[0][:], ACT.Sigmoid, scale=-1.0)
         nc.scalar.activation(carry[:, second], acc_g[1][:], ACT.Sigmoid, scale=-1.0)
-        for cols in on_gpsimd:
-            nc.scalar.activation(picked[:, cols], res_tab[:].indirect(entries(cols.start, cols.stop)), ACT.Copy)
-        nc.vector.tensor_tensor(passed[:, lead], res_tab[:].indirect(entries(lead.start, lead.stop)), lead_carry, ALU.mult)
-        nc.vector.tensor_tensor(passed[:, fused], res_tab[:].indirect(entries(fused.start, fused.stop)), carry[:, fused], ALU.mult)
-        for cols in on_gpsimd:
+        for cols in quarters[1:]:
+            nc.scalar.activation(picked[:, cols], res_tab[:].indirect(entries(cols)), ACT.Copy)
+        nc.vector.tensor_tensor(passed[:, lead], res_tab[:].indirect(entries(lead)), lead_carry, ALU.mult)
+        nc.vector.tensor_tensor(passed[:, fused], res_tab[:].indirect(entries(fused)), carry[:, fused], ALU.mult)
+        for cols in quarters[1:3]:
             nc.gpsimd.tensor_tensor(passed[:, cols], picked[:, cols], carry[:, cols], ALU.mult)
         for h, cols in enumerate(halves):
             nc.vector.scalar_tensor_tensor(gated[:, cols], carry[:, cols], 1.0, acc_y[h][:], ALU.subtract, ALU.mult)
+        nc.vector.tensor_tensor(passed[:, quarters[3]], picked[:, quarters[3]], carry[:, quarters[3]], ALU.mult)
         for cols in halves:
             o = sb.tile([P, H], F32, name=f"result{cols.start}", align_bytes=4 * H)
             nc.vector.scalar_tensor_tensor(o[:], gated[:, cols], 0.0, passed[:, cols], ALU.max, ALU.add)

@@ -79,10 +79,7 @@ def tile_picked_highway_relu_p_kernel(tc, x_words, x_scales, res, w1, w2, offs, 
         def round_weights(name, z, shares):
             g = sb.tile([P, N, PACK], BF16, name=f"grouped_{name}{z}", align_bytes=ALIGN)
             for cast, lo, hi in shares:
-                cast(
-                    g[:, lo:hi, :].rearrange("p (c i) t -> p c t i", i=4),
-                    raw[name, z][:, :, lo:hi].rearrange("p t (c i) -> p c t i", i=4),
-                )
+                cast(g[:, lo:hi, :], raw[name, z][:, :, lo:hi])
             grouped[name, z] = g
 
         def quantise(name, z):
@@ -112,65 +109,69 @@ def tile_picked_highway_relu_p_kernel(tc, x_words, x_scales, res, w1, w2, offs, 
                 stop=(z == PASSES - 1 and closes),
             )
 
+        def in_fours(dst, src):
+            return dst.rearrange("p (c i) t -> p c t i", i=4), src.rearrange("p t (c i) -> p c t i", i=4)
+
+        def plain_on_scalar(dst, src):
+            nc.scalar.copy(*in_fours(dst, src))
+
+        def plain_on_vector(dst, src):
+            nc.vector.tensor_copy(*in_fours(dst, src))
+
         def negated_on_scalar(dst, src):
-            nc.scalar.activation(dst, src, ACT.Copy, scale=-1.0)
+            nc.scalar.activation(*in_fours(dst, src), ACT.Copy, scale=-1.0)
 
-        def negated_on_gpsimd(dst, src):
-            nc.gpsimd.tensor_scalar(dst, src, -1.0, 0.0, ALU.mult, ALU.add)
+        def negated_on_vector(dst, src):
+            nc.vector.tensor_scalar(*in_fours(dst, src), -1.0, None, ALU.mult)
 
-        acc_g = [ps.tile([P, H], F32, name=f"acc_g{h}") for h in range(HALVES)]
-        acc_y = [ps.tile([P, H], F32, name=f"acc_y{h}") for h in range(HALVES)]
         halves = [slice(h * H, (h + 1) * H) for h in range(HALVES)]
         quarters = [slice(q * Q, (q + 1) * Q) for q in range(4)]
-        first, second = halves
-        shared = [(negated_on_scalar, 0, ON_SCALAR), (negated_on_gpsimd, ON_SCALAR, N)]
+        pieces = [quarters[0], slice(Q, 3 * Q), quarters[3]]
+        acc_g = [ps.tile([P, cols.stop - cols.start], F32, name=f"acc_g{cols.start}") for cols in pieces]
+        acc_y = [ps.tile([P, H], F32, name=f"acc_y{h}") for h in range(HALVES)]
+        x_codes = [sb.tile([P, S], U32, name=f"x_codes{z}", align_bytes=ALIGN) for z in range(PASSES)]
 
-        codes0 = sb.tile([P, S], U32, name="codes0", align_bytes=ALIGN)
-        codes1 = sb.tile([P, 3 * Q], U32, name="codes1", align_bytes=ALIGN)
-
-        round_weights("g", 0, [(nc.vector.tensor_copy, 0, N)])
+        round_weights("g", 0, [(plain_on_vector, 0, N)])
         quantise("g", 0)
         nc.vector.tensor_copy(x_sc[:], scale_tab[:].indirect(offsets[:]))
-        gather_words(codes0[:], 0, slice(0, S))
-        for h, cols in enumerate(halves):
-            multiply(acc_g[h][:], "g", 0, codes0[:, cols], cols)
-        round_weights("g", 1, [(nc.scalar.copy, 0, N)])
+        gather_words(x_codes[0][:], 0, slice(0, S))
+        for acc, cols in zip(acc_g, pieces):
+            multiply(acc[:], "g", 0, x_codes[0][:, cols], cols)
+        round_weights("g", 1, [(plain_on_scalar, 0, N)])
         quantise("g", 1)
-        gather_words(codes1[:, first], 1, first)
-        multiply(acc_g[0][:], "g", 1, codes1[:, first], first)
-        gather_words(codes1[:, quarters[2]], 1, quarters[2])
-        multiply(acc_g[1][:, :Q], "g", 1, codes1[:, quarters[2]], quarters[2], closes=False)
-        round_weights("y", 0, shared)
-        quantise("y", 0)
-        multiply(acc_y[0][:], "y", 0, codes0[:, first], first)
-        codes1_last = sb.tile([P, Q], U32, name="codes1_last", tag="raw_y0", align_bytes=RAW_ROW)
-        gather_words(codes1_last[:], 1, quarters[3])
-        multiply(acc_g[1][:, Q:], "g", 1, codes1_last[:], quarters[3])
-        multiply(acc_y[1][:], "y", 0, codes0[:, second], second)
-        round_weights("y", 1, shared)
-        quantise("y", 1)
-        multiply(acc_y[0][:], "y", 1, codes1[:, first], first)
-        multiply(acc_y[1][:, :Q], "y", 1, codes1[:, quarters[2]], quarters[2], closes=False)
-        multiply(acc_y[1][:, Q:], "y", 1, codes1_last[:], quarters[3])
+        for acc, cols in zip(acc_g, pieces):
+            gather_words(x_codes[1][:, cols], 1, cols)
+            multiply(acc[:], "g", 1, x_codes[1][:, cols], cols)
+        shares = ([(negated_on_scalar, 0, N)], [(negated_on_scalar, 0, ON_SCALAR), (negated_on_vector, ON_SCALAR, N)])
+        for z in range(PASSES):
+            round_weights("y", z, shares[z])
+            quantise("y", z)
+            for acc, cols in zip(acc_y, halves):
+                multiply(acc[:], "y", z, x_codes[z][:, cols], cols)
 
-        late = sb.tile([P, 2 * S], F32, name="late", tag="raw_y1", align_bytes=RAW_ROW)
-        carry, gated = late[:, :S], late[:, S:]
-        picked = sb.tile([P, S], F32, name="picked", align_bytes=ALIGN)
+        late = sb.tile([P, 3 * S + LEAD], F32, name="late", tag="raw_y0", align_bytes=RAW_ROW)
+        carry, gated, picked_last = late[:, :S], late[:, S : 2 * S], late[:, 2 * S : 2 * S + Q]
+        lead_at = [S - LEAD // 2, 2 * S]
+        span = lead_at[1] - lead_at[0]
+        lead_pair = late[:, lead_at[0] : lead_at[0] + 2 * span].rearrange("p (a b) -> p a b", a=2)[:, :, :LEAD]
+        picked = sb.tile([P, 3 * Q], F32, name="picked", align_bytes=ALIGN)
         passed = sb.tile([P, S], F32, name="passed", align_bytes=ALIGN)
-        lead, fused = slice(0, LEAD), slice(LEAD, Q)
-        lead_carry = gated[:, H - LEAD // 2 : H + LEAD // 2]
-        nc.scalar.activation(lead_carry, acc_g[0][:, lead], ACT.Sigmoid, scale=-1.0)
-        nc.scalar.activation(carry[:, first], acc_g[0][:], ACT.Sigmoid, scale=-1.0)
-        nc.scalar.activation(carry[:, second], acc_g[1][:], ACT.Sigmoid, scale=-1.0)
-        for cols in quarters[1:]:
-            nc.scalar.activation(picked[:, cols], res_tab[:].indirect(entries(cols)), ACT.Copy)
-        nc.vector.tensor_tensor(passed[:, lead], res_tab[:].indirect(entries(lead)), lead_carry, ALU.mult)
+        nc.scalar.activation(lead_pair, acc_g[0][:].rearrange("p (a b) -> p a b", a=2), ACT.Sigmoid, scale=-1.0)
+        for acc, cols in zip(acc_g[:2], pieces[:2]):
+            nc.scalar.activation(carry[:, cols], acc[:], ACT.Sigmoid, scale=-1.0)
+        for i, at in enumerate(lead_at):
+            cols = slice(i * LEAD, (i + 1) * LEAD)
+            nc.vector.tensor_tensor(passed[:, cols], res_tab[:].indirect(entries(cols)), late[:, at : at + LEAD], ALU.mult)
+        fused = slice(Q, Q + LEAD)
         nc.vector.tensor_tensor(passed[:, fused], res_tab[:].indirect(entries(fused)), carry[:, fused], ALU.mult)
-        for cols in quarters[1:3]:
+        for cols in (slice(fused.stop, fused.stop + Q), slice(fused.stop + Q, 3 * Q)):
+            nc.scalar.activation(picked[:, cols], res_tab[:].indirect(entries(cols)), ACT.Copy)
             nc.gpsimd.tensor_tensor(passed[:, cols], picked[:, cols], carry[:, cols], ALU.mult)
+        nc.scalar.activation(carry[:, quarters[3]], acc_g[2][:], ACT.Sigmoid, scale=-1.0)
+        nc.scalar.activation(picked_last, res_tab[:].indirect(entries(quarters[3])), ACT.Copy)
         for h, cols in enumerate(halves):
             nc.vector.scalar_tensor_tensor(gated[:, cols], carry[:, cols], 1.0, acc_y[h][:], ALU.subtract, ALU.mult)
-        nc.vector.tensor_tensor(passed[:, quarters[3]], picked[:, quarters[3]], carry[:, quarters[3]], ALU.mult)
+        nc.vector.tensor_tensor(passed[:, quarters[3]], picked_last, carry[:, quarters[3]], ALU.mult)
         for cols in halves:
             o = sb.tile([P, H], F32, name=f"result{cols.start}", align_bytes=4 * H)
             nc.vector.scalar_tensor_tensor(o[:], gated[:, cols], 0.0, passed[:, cols], ALU.max, ALU.add)

@@ -26,7 +26,10 @@ LIST_COLS = 16
 ALIGN = 256
 RAW_ROW = 4 * PACK * N
 LEAD = 64
-ON_SCALAR = 64
+FUSED = 192
+ON_SCALAR = 96
+ON_GPSIMD = 48
+FIRST = 16
 
 
 def tile_picked_highway_relu_p_kernel(tc, x_words, x_scales, res, w1, w2, offs, out):
@@ -44,6 +47,9 @@ def tile_picked_highway_relu_p_kernel(tc, x_words, x_scales, res, w1, w2, offs, 
         warm_out = sb.tile([P, 8], F32, name="warm_out")
         nc.vector.memset(warm_in[:], 0.0)
         nc.scalar.activation(warm_out[:], warm_in[:], ACT.Sigmoid)
+
+        minus_one = sb.tile([P, 1], F32, name="minus_one", tag="late", align_bytes=ALIGN)
+        nc.vector.memset(minus_one[:], -1.0)
 
         word_tab, raw = {}, {}
 
@@ -121,12 +127,18 @@ def tile_picked_highway_relu_p_kernel(tc, x_words, x_scales, res, w1, w2, offs, 
         def negated_on_scalar(dst, src):
             nc.scalar.activation(*in_fours(dst, src), ACT.Copy, scale=-1.0)
 
+        def negated_by_tile(dst, src):
+            nc.scalar.activation(*in_fours(dst, src), ACT.Copy, scale=minus_one[:])
+
+        def negated_on_gpsimd(dst, src):
+            nc.gpsimd.tensor_scalar(dst, src.rearrange("p t m -> p m t"), -1.0, 0.0, ALU.mult, ALU.add)
+
         def negated_on_vector(dst, src):
             nc.vector.tensor_scalar(*in_fours(dst, src), -1.0, None, ALU.mult)
 
         halves = [slice(h * H, (h + 1) * H) for h in range(HALVES)]
         quarters = [slice(q * Q, (q + 1) * Q) for q in range(4)]
-        pieces = [quarters[0], slice(Q, 3 * Q), quarters[3]]
+        pieces = [halves[0], quarters[2], quarters[3]]
         acc_g = [ps.tile([P, cols.stop - cols.start], F32, name=f"acc_g{cols.start}") for cols in pieces]
         acc_y = [ps.tile([P, H], F32, name=f"acc_y{h}") for h in range(HALVES)]
         x_codes = [sb.tile([P, S], U32, name=f"x_codes{z}", align_bytes=ALIGN) for z in range(PASSES)]
@@ -142,36 +154,35 @@ def tile_picked_highway_relu_p_kernel(tc, x_words, x_scales, res, w1, w2, offs, 
         for acc, cols in zip(acc_g, pieces):
             gather_words(x_codes[1][:, cols], 1, cols)
             multiply(acc[:], "g", 1, x_codes[1][:, cols], cols)
-        shares = ([(negated_on_scalar, 0, N)], [(negated_on_scalar, 0, ON_SCALAR), (negated_on_vector, ON_SCALAR, N)])
+        shares = (
+            [(negated_on_scalar, 0, N - ON_GPSIMD), (negated_on_gpsimd, N - ON_GPSIMD, N)],
+            [(negated_by_tile, 0, FIRST), (negated_on_scalar, FIRST, ON_SCALAR), (negated_on_vector, ON_SCALAR, N)],
+        )
         for z in range(PASSES):
             round_weights("y", z, shares[z])
             quantise("y", z)
             for acc, cols in zip(acc_y, halves):
                 multiply(acc[:], "y", z, x_codes[z][:, cols], cols)
 
-        late = sb.tile([P, 3 * S + LEAD], F32, name="late", tag="raw_y0", align_bytes=RAW_ROW)
-        carry, gated, picked_last = late[:, :S], late[:, S : 2 * S], late[:, 2 * S : 2 * S + Q]
-        lead_at = [S - LEAD // 2, 2 * S]
-        span = lead_at[1] - lead_at[0]
-        lead_pair = late[:, lead_at[0] : lead_at[0] + 2 * span].rearrange("p (a b) -> p a b", a=2)[:, :, :LEAD]
-        picked = sb.tile([P, 3 * Q], F32, name="picked", align_bytes=ALIGN)
+        late = sb.tile([P, 2 * S], F32, name="late", tag="late", align_bytes=ALIGN)
+        carry, gated = late[:, :S], late[:, S:]
+        picked = sb.tile([P, S], F32, name="picked", align_bytes=ALIGN)
         passed = sb.tile([P, S], F32, name="passed", align_bytes=ALIGN)
-        nc.scalar.activation(lead_pair, acc_g[0][:].rearrange("p (a b) -> p a b", a=2), ACT.Sigmoid, scale=-1.0)
-        for acc, cols in zip(acc_g[:2], pieces[:2]):
+        lead, fused, last = slice(0, LEAD), slice(LEAD, FUSED), quarters[3]
+        on_gpsimd = [slice(FUSED, H), quarters[2]]
+        lead_carry = gated[:, H - LEAD // 2 : H + LEAD // 2]
+        nc.scalar.activation(lead_carry, acc_g[0][:, lead], ACT.Sigmoid, scale=-1.0)
+        for acc, cols in zip(acc_g, pieces):
             nc.scalar.activation(carry[:, cols], acc[:], ACT.Sigmoid, scale=-1.0)
-        for i, at in enumerate(lead_at):
-            cols = slice(i * LEAD, (i + 1) * LEAD)
-            nc.vector.tensor_tensor(passed[:, cols], res_tab[:].indirect(entries(cols)), late[:, at : at + LEAD], ALU.mult)
-        fused = slice(Q, Q + LEAD)
-        nc.vector.tensor_tensor(passed[:, fused], res_tab[:].indirect(entries(fused)), carry[:, fused], ALU.mult)
-        for cols in (slice(fused.stop, fused.stop + Q), slice(fused.stop + Q, 3 * Q)):
+        for cols in on_gpsimd + [last]:
             nc.scalar.activation(picked[:, cols], res_tab[:].indirect(entries(cols)), ACT.Copy)
+        nc.vector.tensor_tensor(passed[:, lead], res_tab[:].indirect(entries(lead)), lead_carry, ALU.mult)
+        nc.vector.tensor_tensor(passed[:, fused], res_tab[:].indirect(entries(fused)), carry[:, fused], ALU.mult)
+        for cols in on_gpsimd:
             nc.gpsimd.tensor_tensor(passed[:, cols], picked[:, cols], carry[:, cols], ALU.mult)
-        nc.scalar.activation(carry[:, quarters[3]], acc_g[2][:], ACT.Sigmoid, scale=-1.0)
-        nc.scalar.activation(picked_last, res_tab[:].indirect(entries(quarters[3])), ACT.Copy)
         for h, cols in enumerate(halves):
             nc.vector.scalar_tensor_tensor(gated[:, cols], carry[:, cols], 1.0, acc_y[h][:], ALU.subtract, ALU.mult)
-        nc.vector.tensor_tensor(passed[:, quarters[3]], picked_last, carry[:, quarters[3]], ALU.mult)
+        nc.vector.tensor_tensor(passed[:, last], picked[:, last], carry[:, last], ALU.mult)
         for cols in halves:
             o = sb.tile([P, H], F32, name=f"result{cols.start}", align_bytes=4 * H)
             nc.vector.scalar_tensor_tensor(o[:], gated[:, cols], 0.0, passed[:, cols], ALU.max, ALU.add)

@@ -26,7 +26,7 @@ LIST_COLS = 16
 ALIGN = 256
 RAW_ROW = 4 * PACK * N
 LEAD = 64
-FUSED = 192
+FUSED = 224
 ON_SCALAR = 96
 ON_GPSIMD = 48
 FIRST = 16
@@ -168,8 +168,8 @@ def tile_picked_highway_relu_p_kernel(tc, x_words, x_scales, res, w1, w2, offs, 
         carry, gated = late[:, :S], late[:, S:]
         picked = sb.tile([P, S], F32, name="picked", align_bytes=ALIGN)
         passed = sb.tile([P, S], F32, name="passed", align_bytes=ALIGN)
-        lead, fused, last = slice(0, LEAD), slice(LEAD, FUSED), quarters[3]
-        on_gpsimd = [slice(FUSED, H), quarters[2]]
+        lead, fused, last = slice(0, LEAD), slice(LEAD, FUSED), slice(FUSED + LEAD + Q, S)
+        on_gpsimd = [slice(FUSED, FUSED + LEAD), slice(FUSED + LEAD, last.start)]
         lead_carry = gated[:, H - LEAD // 2 : H + LEAD // 2]
         nc.scalar.activation(lead_carry, acc_g[0][:, lead], ACT.Sigmoid, scale=-1.0)
         for acc, cols in zip(acc_g, pieces):

@@ -140,7 +140,7 @@ def tile_picked_highway_relu_p_kernel(tc, x_words, x_scales, res, w1, w2, offs, 
         quarters = [slice(q * Q, (q + 1) * Q) for q in range(4)]
         pieces = [halves[0], quarters[2], quarters[3]]
         acc_g = [ps.tile([P, cols.stop - cols.start], F32, name=f"acc_g{cols.start}") for cols in pieces]
-        acc_y = [ps.tile([P, H], F32, name=f"acc_y{h}") for h in range(HALVES)]
+        acc_y = [ps.tile([P, Q], F32, name=f"acc_y{q}") for q in range(4)]
         x_codes = [sb.tile([P, S], U32, name=f"x_codes{z}", align_bytes=ALIGN) for z in range(PASSES)]
 
         round_weights("g", 0, [(plain_on_vector, 0, N)])
@@ -161,27 +161,29 @@ def tile_picked_highway_relu_p_kernel(tc, x_words, x_scales, res, w1, w2, offs, 
         for z in range(PASSES):
             round_weights("y", z, shares[z])
             quantise("y", z)
-            for acc, cols in zip(acc_y, halves):
+            for acc, cols in zip(acc_y, quarters):
                 multiply(acc[:], "y", z, x_codes[z][:, cols], cols)
 
         late = sb.tile([P, 2 * S], F32, name="late", tag="late", align_bytes=ALIGN)
         carry, gated = late[:, :S], late[:, S:]
         picked = sb.tile([P, S], F32, name="picked", align_bytes=ALIGN)
         passed = sb.tile([P, S], F32, name="passed", align_bytes=ALIGN)
-        lead, fused, last = slice(0, LEAD), slice(LEAD, FUSED), slice(FUSED + LEAD + Q, S)
+        fused, last = slice(2 * LEAD, FUSED), slice(FUSED + LEAD + Q, S)
         on_gpsimd = [slice(FUSED, FUSED + LEAD), slice(FUSED + LEAD, last.start)]
-        lead_carry = gated[:, H - LEAD // 2 : H + LEAD // 2]
-        nc.scalar.activation(lead_carry, acc_g[0][:, lead], ACT.Sigmoid, scale=-1.0)
+        lead_pair = gated.rearrange("p (h c) -> p h c", h=HALVES)[:, :, Q - LEAD // 2 : Q + LEAD // 2]
+        nc.scalar.activation(lead_pair, acc_g[0][:, : 2 * LEAD].rearrange("p (h c) -> p h c", h=HALVES), ACT.Sigmoid, scale=-1.0)
         for acc, cols in zip(acc_g, pieces):
             nc.scalar.activation(carry[:, cols], acc[:], ACT.Sigmoid, scale=-1.0)
         for cols in on_gpsimd + [last]:
             nc.scalar.activation(picked[:, cols], res_tab[:].indirect(entries(cols)), ACT.Copy)
-        nc.vector.tensor_tensor(passed[:, lead], res_tab[:].indirect(entries(lead)), lead_carry, ALU.mult)
+        for h in range(HALVES):
+            lead = slice(h * LEAD, (h + 1) * LEAD)
+            nc.vector.tensor_tensor(passed[:, lead], res_tab[:].indirect(entries(lead)), lead_pair[:, h, :], ALU.mult)
         nc.vector.tensor_tensor(passed[:, fused], res_tab[:].indirect(entries(fused)), carry[:, fused], ALU.mult)
         for cols in on_gpsimd:
             nc.gpsimd.tensor_tensor(passed[:, cols], picked[:, cols], carry[:, cols], ALU.mult)
-        for h, cols in enumerate(halves):
-            nc.vector.scalar_tensor_tensor(gated[:, cols], carry[:, cols], 1.0, acc_y[h][:], ALU.subtract, ALU.mult)
+        for acc, cols in zip(acc_y, quarters):
+            nc.vector.scalar_tensor_tensor(gated[:, cols], carry[:, cols], 1.0, acc[:], ALU.subtract, ALU.mult)
         nc.vector.tensor_tensor(passed[:, last], picked[:, last], carry[:, last], ALU.mult)
         for cols in halves:
             o = sb.tile([P, H], F32, name=f"result{cols.start}", align_bytes=4 * H)

from contextlib import ExitStack

import concourse.mybir as mybir

K, T, S, N = 1024, 1024, 512, 128
FLOPS = 2 * 2 * K * N * S

F32 = mybir.dt.float32
BF16 = mybir.dt.bfloat16
I32 = mybir.dt.int32
U32 = mybir.dt.uint32
U16 = mybir.dt.uint16
U8 = mybir.dt.uint8
FP8X4 = mybir.dt.float8_e4m3fn_x4
ACT = mybir.ActivationFunctionType
ALU = mybir.AluOpType

P = 128
PACK = 4
K_PASS = P * PACK
PASSES = K // K_PASS
HALVES = 2
H = S // HALVES
Q = S // 4
LIST_COLS = 16
ALIGN = 256
RAW_ROW = 4 * PACK * N
LEAD = 64
FUSED = 224
ON_SCALAR = 96
ON_GPSIMD = 48
FIRST = 16


def tile_picked_highway_relu_p_kernel(tc, x_words, x_scales, res, w1, w2, offs, out):
    nc = tc.nc
    with ExitStack() as ctx:
        sb = ctx.enter_context(tc.tile_pool(name="sb", bufs=1))
        ps = ctx.enter_context(tc.psum_pool(name="ps", bufs=1))

        offsets = sb.tile([P, S // LIST_COLS], U16, name="offsets")

        scale_tab = sb.tile([P, T], U8, name="scale_tab", align_bytes=T)
        nc.vector.memset(scale_tab[:].bitcast(I32), 0)

        warm_in = sb.tile([P, 8], F32, name="warm_in")
        warm_out = sb.tile([P, 8], F32, name="warm_out")
        nc.vector.memset(warm_in[:], 0.0)
        nc.scalar.activation(warm_out[:], warm_in[:], ACT.Sigmoid)

        minus_one = sb.tile([P, 1], F32, name="minus_one", tag="late", align_bytes=ALIGN)
        nc.vector.memset(minus_one[:], -1.0)

        word_tab, raw = {}, {}

        def load_words(z):
            tab = sb.tile([P, T], I32, name=f"word_tab{z}", align_bytes=4 * T)
            nc.sync.dma_start(tab[:], x_words[z].rearrange("p c r -> p (c r)").bitcast(I32))
            word_tab[z] = tab

        def load_weights(name, w, z):
            t = sb.tile([P, PACK, N], F32, name=f"raw_{name}{z}", tag=f"raw_{name}{z}", align_bytes=RAW_ROW)
            nc.sync.dma_start(t[:], w[z * K_PASS : (z + 1) * K_PASS, :].rearrange("(p j) m -> p j m", j=PACK))
            raw[name, z] = t

        load_weights("g", w2, 0)
        nc.sync.dma_start(offsets[:], offs)
        scales_i32 = x_scales.bitcast(I32)
        for q in range(4):
            nc.sync.dma_start(
                scale_tab[32 * q : 32 * q + 4 * PASSES, :].bitcast(I32),
                scales_i32[:, 4 * q : 4 * q + 4, :],
            )
        load_words(0)
        load_weights("g", w2, 1)
        load_words(1)
        for z in range(PASSES):
            load_weights("y", w1, z)
        res_tab = sb.tile([P, T], F32, name="res_tab", align_bytes=4 * T)
        nc.sync.dma_start(res_tab[:], res)

        x_sc = sb.tile([P, S], U8, name="x_sc", align_bytes=ALIGN)
        w_codes, w_scales, grouped = {}, {}, {}

        def round_weights(name, z, shares):
            g = sb.tile([P, N, PACK], BF16, name=f"grouped_{name}{z}", align_bytes=ALIGN)
            for cast, lo, hi in shares:
                cast(g[:, lo:hi, :], raw[name, z][:, :, lo:hi])
            grouped[name, z] = g

        def quantise(name, z):
            codes = sb.tile([P, N], U32, name=f"w_codes_{name}{z}", align_bytes=ALIGN)
            scales = sb.tile([P, N], U8, name=f"w_scales_{name}{z}", align_bytes=ALIGN)
            nc.vector.quantize_mx(
                out=codes[:].bitcast(FP8X4),
                scales=scales[:],
                in_=grouped[name, z][:].rearrange("p m t -> p (m t)"),
            )
            w_codes[name, z], w_scales[name, z] = codes, scales

        def entries(cols):
            return offsets[:, cols.start // LIST_COLS : cols.stop // LIST_COLS]

        def gather_words(codes, z, cols):
            nc.vector.tensor_copy(codes, word_tab[z][:].bitcast(U32).indirect(entries(cols)))

        def multiply(acc, name, z, codes, cols, closes=True):
            nc.tensor.matmul_mx(
                out=acc,
                lhsT=w_codes[name, z][:].bitcast(FP8X4),
                lhsT_scale=w_scales[name, z][:],
                rhs=codes.bitcast(FP8X4),
                rhs_scale=x_sc[4 * z : P, cols],
                start=(z == 0),
                stop=(z == PASSES - 1 and closes),
            )

        def in_fours(dst, src):
            return dst.rearrange("p (c i) t -> p c t i", i=4), src.rearrange("p t (c i) -> p c t i", i=4)

        def plain_on_scalar(dst, src):
            nc.scalar.copy(*in_fours(dst, src))

        def plain_on_vector(dst, src):
            nc.vector.tensor_copy(*in_fours(dst, src))

        def negated_on_scalar(dst, src):
            nc.scalar.activation(*in_fours(dst, src), ACT.Copy, scale=-1.0)

        def negated_by_tile(dst, src):
            nc.scalar.activation(*in_fours(dst, src), ACT.Copy, scale=minus_one[:])

        def negated_on_gpsimd(dst, src):
            nc.gpsimd.tensor_scalar(dst, src.rearrange("p t m -> p m t"), -1.0, 0.0, ALU.mult, ALU.add)

        def negated_on_vector(dst, src):
            nc.vector.tensor_scalar(*in_fours(dst, src), -1.0, None, ALU.mult)

        halves = [slice(h * H, (h + 1) * H) for h in range(HALVES)]
        quarters = [slice(q * Q, (q + 1) * Q) for q in range(4)]
        pieces = [halves[0], quarters[2], quarters[3]]
        acc_g = [ps.tile([P, cols.stop - cols.start], F32, name=f"acc_g{cols.start}") for cols in pieces]
        acc_y = [ps.tile([P, Q], F32, name=f"acc_y{q}") for q in range(4)]
        x_codes = [sb.tile([P, S], U32, name=f"x_codes{z}", align_bytes=ALIGN) for z in range(PASSES)]

        round_weights("g", 0, [(plain_on_vector, 0, N)])
        quantise("g", 0)
        nc.vector.tensor_copy(x_sc[:], scale_tab[:].indirect(offsets[:]))
        gather_words(x_codes[0][:], 0, slice(0, S))
        for acc, cols in zip(acc_g, pieces):
            multiply(acc[:], "g", 0, x_codes[0][:, cols], cols)
        round_weights("g", 1, [(plain_on_scalar, 0, N)])
        quantise("g", 1)
        for acc, cols in zip(acc_g, pieces):
            gather_words(x_codes[1][:, cols], 1, cols)
            multiply(acc[:], "g", 1, x_codes[1][:, cols], cols)
        shares = (
            [(negated_on_scalar, 0, N - ON_GPSIMD), (negated_on_gpsimd, N - ON_GPSIMD, N)],
            [(negated_by_tile, 0, FIRST), (negated_on_scalar, FIRST, ON_SCALAR), (negated_on_vector, ON_SCALAR, N)],
        )
        for z in range(PASSES):
            round_weights("y", z, shares[z])
            quantise("y", z)
            for acc, cols in zip(acc_y, quarters):
                multiply(acc[:], "y", z, x_codes[z][:, cols], cols)

        late = sb.tile([P, 2 * S], F32, name="late", tag="late", align_bytes=ALIGN)
        carry, gated = late[:, :S], late[:, S:]
        picked = sb.tile([P, S], F32, name="picked", align_bytes=ALIGN)
        passed = sb.tile([P, S], F32, name="passed", align_bytes=ALIGN)
        fused, last = slice(2 * LEAD, FUSED), slice(FUSED + LEAD + Q, S)
        on_gpsimd = [slice(FUSED, FUSED + LEAD), slice(FUSED + LEAD, last.start)]
        lead_pair = gated.rearrange("p (h c) -> p h c", h=HALVES)[:, :, Q - LEAD // 2 : Q + LEAD // 2]
        nc.scalar.activation(lead_pair, acc_g[0][:, : 2 * LEAD].rearrange("p (h c) -> p h c", h=HALVES), ACT.Sigmoid, scale=-1.0)
        for acc, cols in zip(acc_g, pieces):
            nc.scalar.activation(carry[:, cols], acc[:], ACT.Sigmoid, scale=-1.0)
        for cols in on_gpsimd + [last]:
            nc.scalar.activation(picked[:, cols], res_tab[:].indirect(entries(cols)), ACT.Copy)
        for h in range(HALVES):
            lead = slice(h * LEAD, (h + 1) * LEAD)
            nc.vector.tensor_tensor(passed[:, lead], res_tab[:].indirect(entries(lead)), lead_pair[:, h, :], ALU.mult)
        nc.vector.tensor_tensor(passed[:, fused], res_tab[:].indirect(entries(fused)), carry[:, fused], ALU.mult)
        for cols in on_gpsimd:
            nc.gpsimd.tensor_tensor(passed[:, cols], picked[:, cols], carry[:, cols], ALU.mult)
        for acc, cols in zip(acc_y, quarters):
            nc.vector.scalar_tensor_tensor(gated[:, cols], carry[:, cols], 1.0, acc[:], ALU.subtract, ALU.mult)
        nc.vector.tensor_tensor(passed[:, last], picked[:, last], carry[:, last], ALU.mult)
        for cols in halves:
            o = sb.tile([P, H], F32, name=f"result{cols.start}", align_bytes=4 * H)
            nc.vector.scalar_tensor_tensor(o[:], gated[:, cols], 0.0, passed[:, cols], ALU.max, ALU.add)
            nc.sync.dma_start(out[:, cols], o[:])
